import numpy as np
import ml_dtypes


def mxq(x, axis, fmt="e4m3"):
    dtype, down = {"e4m3": (ml_dtypes.float8_e4m3fn, 7), "e5m2": (ml_dtypes.float8_e5m2, 14)}[fmt]
    v = np.moveaxis(np.asarray(x, np.float32).astype(ml_dtypes.bfloat16).astype(np.float64), axis, -1)
    blocks = v.reshape(v.shape[:-1] + (-1, 32))
    amax = np.abs(blocks).max(-1, keepdims=True)
    byte = np.maximum(np.where(amax > 0, np.frexp(amax)[1] - 1 + 127, 0) - down, 1)
    scale = np.exp2(byte - 127.0)
    codes = (blocks / scale).astype(np.float32).astype(dtype).astype(np.float64)
    return np.moveaxis((codes * scale).reshape(v.shape), -1, axis)


WIDE = False


def mx_kscale(k):
    if not WIDE:
        return np.ones(k)
    levels = np.array([10, -10, 5, -5, 0])
    if k % 512:
        return np.exp2(np.random.permutation(np.resize(levels, k // 32))).repeat(32)
    a = np.empty((k // 512, 16))
    for p in range(k // 512):
        a[p, :8] = np.random.permutation(np.resize(levels, 8))
        for g in range(8):
            far = levels[np.abs(levels - a[p, g]) >= 10]
            a[p, g + 8] = far[np.random.randint(len(far))]
    return np.exp2(a.ravel()).repeat(32)


def f64(x):
    return np.asarray(x).astype(np.float64)


def striped(idx):
    return np.tile(idx.reshape(-1, 16).T, (8, 1)).astype(np.uint16)


def unstriped(offs):
    return offs[:16].T.reshape(-1).astype(np.int64)


def striped8(idx):
    return np.concatenate([x.reshape(-1, 16).T for x in idx]).astype(np.uint16)


def runs(offs, k):
    lists = np.stack([offs[16 * r : 16 * r + 16].T.reshape(-1) for r in range(8)]).astype(np.int64)
    return lists[np.arange(k) % 512 // 64]


def pack_weight(w):
    k, n = w.shape
    w = f64(np.asarray(w, np.float32).astype(ml_dtypes.bfloat16)).reshape(k // 32, 32, n)
    amax = np.abs(w).max(1)
    byte = np.clip(np.where(amax > 0, np.frexp(amax)[1] - 1 + 127 - 7, 1), 1, 254)
    scaled = (w * np.exp2(127.0 - byte)[:, None, :]).reshape(k, n).astype(np.float32)
    words = np.ascontiguousarray(scaled.reshape(k // 512, 128, 4, n).transpose(0, 1, 3, 2)).astype(ml_dtypes.float8_e4m3fn).view(np.uint8)
    return words, np.ascontiguousarray(byte.astype(np.uint8).reshape(k // 512, 16, n))


def unpack_weight(words, scales):
    g, p, n, _ = words.shape
    vals = np.ascontiguousarray(words).view(ml_dtypes.float8_e4m3fn).astype(np.float64) * np.repeat(np.exp2(scales.astype(np.float64) - 127.0), 8, axis=1)[..., None]
    return vals.transpose(0, 1, 3, 2).reshape(g * 512, n)


E2M1 = np.array([0.0, 0.5, 1.0, 1.5, 2.0, 3.0, 4.0, 6.0, -0.0, -0.5, -1.0, -1.5, -2.0, -3.0, -4.0, -6.0])


def pack_fp4(w):
    k, n = w.shape
    w = f64(np.asarray(w, np.float32).astype(ml_dtypes.bfloat16)).reshape(k // 32, 32, n)
    amax = np.abs(w).max(1)
    mant, ex = np.frexp(amax / 6.0)
    byte = np.clip(np.where(amax > 0, np.where(mant > 0.5, ex, ex - 1) + 127, 1), 1, 254)
    scaled = (w * np.exp2(127.0 - byte)[:, None, :]).reshape(k, n).astype(np.float32)
    c = np.ascontiguousarray(scaled.reshape(k // 512, 128, 4, n).transpose(0, 1, 3, 2)).astype(ml_dtypes.float4_e2m1fn).view(np.uint8) & 0xF
    words = (c[..., 0::2] | (c[..., 1::2] << 4)).reshape(k // 512, 128, 2 * n)
    return np.ascontiguousarray(words), np.ascontiguousarray(byte.astype(np.uint8).reshape(k // 512, 16, n))


def unpack_fp4(words, scales):
    g, _, n = scales.shape
    words = np.ascontiguousarray(words).reshape(g, 128, n, 2)
    nib = np.empty((g, 128, n, 4), np.uint8)
    nib[..., 0::2] = words & 0xF
    nib[..., 1::2] = words >> 4
    vals = E2M1[nib] * np.repeat(np.exp2(scales.astype(np.float64) - 127.0), 8, axis=1)[..., None]
    return vals.transpose(0, 1, 3, 2).reshape(g * 512, n)


def planes(y):
    n, m = y.shape
    v = y.astype(np.float32).astype(ml_dtypes.bfloat16).astype(np.float64).reshape(n // 32, 32, m)
    top = np.abs(v).max(1)
    byte = np.clip(np.where(top > 0, np.frexp(top)[1] - 1 + 127 - 7, 1), 1, 254)
    codes = (v * np.exp2(127.0 - byte)[:, None, :]).reshape(n, m).astype(np.float32).astype(ml_dtypes.float8_e4m3fn).view(np.uint8)
    words = codes.reshape(n // 512, 128, 4, m).transpose(0, 1, 3, 2)
    return np.ascontiguousarray(words), np.ascontiguousarray(byte.astype(np.uint8).reshape(n // 512, 16, m))


K, T, S, H, V = 512, 2048, 1024, 512, 512


def setup_inputs():
    n = np.random.standard_normal
    s = mx_kscale(K)[:, None]
    u = mx_kscale(H)
    packed_xT = pack_weight(n((K, T)) * s)
    packed_w2 = pack_fp4(n((H, H)) / np.sqrt(H) / u[:, None])
    return {
        "x_words": packed_xT[0],
        "x_scales": packed_xT[1],
        "w1": (n((K, H)) / np.sqrt(K) / s * u).astype(np.float32),
        "w2_words": packed_w2[0],
        "w2_scales": packed_w2[1],
        "offs": striped8(np.stack([np.random.permutation(T)[:S] for _ in range(8)])),
        "left": striped(np.random.permutation(S)[:V]),
        "right": striped(np.random.permutation(S)[:V]),
    }


def reference(x_words, x_scales, w1, w2_words, w2_scales, offs, left, right):
    xq = unpack_weight(x_words, x_scales)[np.arange(K)[:, None], runs(offs, K)]
    h = mxq(f64(w1), 0, "e4m3").T @ xq
    z = np.abs(h[:, unstriped(left)] - h[:, unstriped(right)])
    out_0 = unpack_fp4(w2_words, w2_scales).T @ mxq(z, 0, "e4m3")
    return (out_0,) + planes(out_0)

@@ -1,0 +1,206 @@
+from contextlib import ExitStack
+
+import concourse.mybir as mybir
+
+K, T, S, H, V = 512, 2048, 1024, 512, 512
+FLOPS = 2 * K * H * S + 2 * H * H * V
+
+F32 = mybir.dt.float32
+BF16 = mybir.dt.bfloat16
+I32 = mybir.dt.int32
+U32 = mybir.dt.uint32
+U16 = mybir.dt.uint16
+U8 = mybir.dt.uint8
+FP8X4 = mybir.dt.float8_e4m3fn_x4
+FP4X4 = mybir.dt.float4_e2m1fn_x4
+ABS = mybir.ActivationFunctionType.Abs
+SUB = mybir.AluOpType.subtract
+
+P = 128
+PACK = 4
+BANK = 512
+BLOCK = 128
+STRETCHES = ((0, 256), (256, 128), (384, 128))
+RING = 3
+
+
+def tile_picked_phpair_abs_po_kernel(
+    tc, x_words, x_scales, w1, w2_words, w2_scales, offs, left, right, out_0, out_1, out_2
+):
+    nc = tc.nc
+    with ExitStack() as ctx:
+        sb = ctx.enter_context(tc.tile_pool(name="sb", bufs=1))
+        ps_h = ctx.enter_context(tc.psum_pool(name="ps_h", bufs=4))
+        ps_o = ctx.enter_context(tc.psum_pool(name="ps_o", bufs=4))
+
+        offs_t = sb.tile([P, S // 16], U16, name="offs_t")
+        left_t = sb.tile([P, V // 16], U16, name="left_t")
+        right_t = sb.tile([P, V // 16], U16, name="right_t")
+        xs_win = sb.tile([P, T], U8, name="xs_win", align_bytes=64)
+        xw_win = sb.tile([P, T], I32, name="xw_win", align_bytes=64)
+        xs_got = sb.tile([P, S], U8, name="xs_got", align_bytes=64)
+        xs_mm = sb.tile([P, S], U8, name="xs_mm", align_bytes=64)
+        w2s_raw = sb.tile([P, H], U8, name="w2s_raw", align_bytes=64)
+        w2w_raw = sb.tile([P, 2 * H], U8, name="w2w_raw", align_bytes=64)
+
+        nc.vector.memset(xs_mm[:].bitcast(I32), 0)
+
+        nc.sync.dma_start(offs_t[:], offs)
+        warm = sb.tile([P, 16], F32, name="warm")
+        nc.vector.memset(warm[:, 0:8], 0.0)
+        nc.scalar.activation(warm[:, 8:16], warm[:, 0:8], ABS)
+        nc.sync.dma_start(
+            xs_win[:].bitcast(I32), x_scales[0].bitcast(I32).unsqueeze(1).to_broadcast([16, 8, T // 4])
+        )
+        nc.sync.dma_start(xw_win[:], x_words[0].rearrange("p n t -> p (n t)").bitcast(I32))
+        nc.sync.dma_start(left_t[:], left)
+        nc.sync.dma_start(right_t[:], right)
+        w1_rows = w1.rearrange("(p j) c -> p j c", j=PACK)
+        w1_raw = []
+        for a in range(2):
+            raw = sb.tile([P, PACK, H // 2], F32, name=f"w1_raw{a}", tag=f"w1_raw{a}", align_bytes=64)
+            nc.sync.dma_start(raw[:], w1_rows[:, :, a * (H // 2) : (a + 1) * (H // 2)])
+            w1_raw.append(raw)
+        nc.sync.dma_start(w2w_raw[:].bitcast(I32), w2_words[0].bitcast(I32))
+        nc.gpsimd.memset(w2s_raw[:].bitcast(I32), 0)
+        for q in range(4):
+            nc.gpsimd.dma_start(
+                w2s_raw[32 * q : 32 * q + 4, :].bitcast(I32), w2_scales[0][4 * q : 4 * q + 4, :].bitcast(I32)
+            )
+
+        nc.vector.tensor_copy(xs_got[:], xs_win[:].indirect(offs_t[:]))
+        for q in range(4):
+            nc.scalar.dma_start(
+                xs_mm[32 * q : 32 * q + 4, :].bitcast(I32), xs_got[32 * q : 32 * q + 32 : 8, :].bitcast(I32)
+            )
+        xw_got = []
+        for a in range(S // BANK):
+            got = sb.tile([P, BANK], I32, name=f"xw_got{a}", align_bytes=64)
+            cols = slice(a * BANK // 16, (a + 1) * BANK // 16)
+            nc.vector.tensor_copy(got[:].bitcast(U32), xw_win[:].bitcast(U32).indirect(offs_t[:, cols]))
+            xw_got.append(got)
+
+        w1_b = sb.tile([P, PACK, P, PACK], BF16, name="w1_b", tag="w1_b", align_bytes=64)
+        for a, cast in enumerate((nc.scalar.copy, nc.vector.tensor_copy)):
+            cast(
+                w1_b[:, :, a * 64 : (a + 1) * 64, :].rearrange("p t m j -> p m j t"),
+                w1_raw[a][:].rearrange("p j (m t) -> p m j t", t=PACK),
+            )
+        w1_q = sb.tile([P, H], I32, name="w1_q", align_bytes=64)
+        w1_s = sb.tile([P, H], U8, name="w1_s", align_bytes=64)
+        for t0, t1 in ((0, 1), (1, 2), (2, 4)):
+            nc.vector.quantize_mx(
+                out=w1_q[:, t0 * P : t1 * P].bitcast(FP8X4),
+                scales=w1_s[:, t0 * P : t1 * P],
+                in_=w1_b[:, t0:t1, :, :].rearrange("p t m j -> p (t m j)"),
+            )
+
+        w2_w = sb.tile([P, 2 * H], U8, name="w2_w", tag="w1_b", align_bytes=64)
+        w2_s = sb.tile([P, H], U8, name="w2_s", tag="w1_raw1", align_bytes=64)
+        nc.vector.tensor_copy(
+            w2_w[:].rearrange("p (t m b) -> p t m b", t=PACK, b=2),
+            w2w_raw[:].rearrange("p (m t b) -> p t m b", t=PACK, b=2),
+        )
+        nc.vector.tensor_copy(
+            w2_s[:].rearrange("p (t m) -> p t m", t=PACK), w2s_raw[:].rearrange("p (m t) -> p t m", t=PACK)
+        )
+
+        h = []
+        for t in range(PACK):
+            plane = sb.tile([P, S], F32, name=f"h{t}")
+            for a in range(S // BANK):
+                cols = slice(a * BANK, (a + 1) * BANK)
+                acc = ps_h.tile([P, BANK], F32, name="acc_h")
+                nc.tensor.matmul_mx(
+                    out=acc[:],
+                    lhsT=w1_q[:, t * P : (t + 1) * P].bitcast(FP8X4),
+                    lhsT_scale=w1_s[:, t * P : (t + 1) * P],
+                    rhs=xw_got[a][:].bitcast(FP8X4),
+                    rhs_scale=xs_mm[:, cols],
+                    start=True,
+                    stop=True,
+                )
+                nc.scalar.copy(plane[:, cols], acc[:])
+            h.append(plane)
+
+        o_q = sb.tile([P, V], I32, name="o_q", align_bytes=64)
+        o_s = sb.tile([P, V], U8, name="o_s", align_bytes=64)
+        out_rows = out_0.rearrange("(p t) v -> p t v", t=PACK)
+        out_words = out_1[0].rearrange("p n t -> p (n t)").bitcast(I32)
+
+        blocks = V // BLOCK
+        diffs = [sb.tile([P, PACK, BLOCK], F32, name=f"diff{b}") for b in range(blocks)]
+        z_in = [sb.tile([P, 2 * BLOCK], F32, name=f"z_in{b}", align_bytes=64) for b in range(blocks)]
+        y_in = [sb.tile([P, 2 * BLOCK], F32, name=f"y_in{b}", align_bytes=64) for b in range(blocks)]
+        spare = [sb.tile([P, 2 * BLOCK], F32, name=f"spare{b}") for b in range(2)]
+        accs = {}
+
+        def pair_of_units(units, buf, halves=(0, 1)):
+            for (b, t), e in zip(units, halves):
+                cols = slice(b * BLOCK // 16, (b + 1) * BLOCK // 16)
+                nc.vector.tensor_copy(buf[:, e * BLOCK : (e + 1) * BLOCK], h[t][:].indirect(right_t[:, cols]))
+            for (b, t), e in zip(units, halves):
+                cols = slice(b * BLOCK // 16, (b + 1) * BLOCK // 16)
+                nc.vector.tensor_tensor(
+                    diffs[b][:, t, :], h[t][:].indirect(left_t[:, cols]), buf[:, e * BLOCK : (e + 1) * BLOCK], SUB
+                )
+
+        def second_layer(b):
+            z_b = z_in[b][:].bitcast(BF16)
+            nc.scalar.activation(
+                z_b.rearrange("p (c i t) -> p c t i", i=4, t=PACK),
+                diffs[b][:].rearrange("p t (c i) -> p c t i", i=4),
+                ABS,
+            )
+            z_q = sb.tile([P, BLOCK], I32, name=f"z_q{b}", align_bytes=64)
+            z_s = sb.tile([P, BLOCK], U8, name=f"z_s{b}", align_bytes=64)
+            nc.vector.quantize_mx(out=z_q[:].bitcast(FP8X4), scales=z_s[:], in_=z_b)
+            acc = ps_o.tile([P, PACK, BLOCK], F32, name="acc_o")
+            for t in range(PACK):
+                nc.tensor.matmul_mx(
+                    out=acc[:, t, :],
+                    lhsT=w2_w[:, 2 * t * P : 2 * (t + 1) * P].bitcast(FP4X4),
+                    lhsT_scale=w2_s[:, t * P : (t + 1) * P],
+                    rhs=z_q[:].bitcast(FP8X4),
+                    rhs_scale=z_s[:],
+                    start=True,
+                    stop=True,
+                )
+            accs[b] = acc
+
+        def hand_out(b):
+            cols = slice(b * BLOCK, (b + 1) * BLOCK)
+            y = sb.tile([P, PACK, BLOCK], F32, name=f"y{b}")
+            nc.scalar.copy(y[:], accs[b][:])
+            nc.sync.dma_start(out_rows[:, :, cols], y[:])
+            y_b = y_in[b][:].bitcast(BF16)
+            if b < 2:
+                nc.scalar.copy(y_b.rearrange("p (c t) -> p c t", t=PACK), accs[b][:].rearrange("p t c -> p c t"))
+            else:
+                nc.vector.tensor_copy(
+                    y_b.rearrange("p (c i t) -> p c t i", i=4, t=PACK), y[:].rearrange("p t (c i) -> p c t i", i=4)
+                )
+            nc.vector.quantize_mx(out=o_q[:, cols].bitcast(FP8X4), scales=o_s[:, cols], in_=y_b)
+
+        pair_of_units(((0, 0), (1, 0)), spare[0])
+        pair_of_units(((0, 1), (1, 1)), spare[1])
+        pair_of_units(((0, 2), (0, 3)), spare[0])
+        second_layer(0)
+        pair_of_units(((1, 2), (1, 3)), spare[0], (1, 0))
+        second_layer(1)
+        hand_out(0)
+        pair_of_units(((2, 0), (2, 1)), z_in[0])
+        hand_out(1)
+        nc.sync.dma_start(out_words[:, 0 : V // 2], o_q[:, 0 : V // 2])
+        pair_of_units(((2, 2), (2, 3)), z_in[1])
+        second_layer(2)
+        pair_of_units(((3, 0), (3, 1)), y_in[0])
+        pair_of_units(((3, 2), (3, 3)), z_in[2])
+        second_layer(3)
+        hand_out(2)
+        hand_out(3)
+        nc.sync.dma_start(out_words[:, V // 2 : V], o_q[:, V // 2 : V])
+
+        for q in range(4):
+            eng = nc.scalar if q % 2 else nc.sync
+            eng.dma_start(out_2[0][4 * q : 4 * q + 4, :].bitcast(I32), o_s[32 * q : 32 * q + 4, :].bitcast(I32))

@@ -18,10 +18,14 @@ SUB = mybir.AluOpType.subtract
 
 P = 128
 PACK = 4
+QUADRANTS = 4
+LIST = 16
 BANK = 512
-BLOCK = 128
-STRETCHES = ((0, 256), (256, 128), (384, 128))
-RING = 3
+H_BANKS = 4
+QUARTER = S // 4
+GROUP = 128
+RUN = 4
+W1_CUTS = (0, 128, 384, H)
 
 
 def tile_picked_phpair_abs_po_kernel(
@@ -30,177 +34,229 @@ def tile_picked_phpair_abs_po_kernel(
     nc = tc.nc
     with ExitStack() as ctx:
         sb = ctx.enter_context(tc.tile_pool(name="sb", bufs=1))
-        ps_h = ctx.enter_context(tc.psum_pool(name="ps_h", bufs=4))
-        ps_o = ctx.enter_context(tc.psum_pool(name="ps_o", bufs=4))
+        ps_h = ctx.enter_context(tc.psum_pool(name="ps_h", bufs=1))
+        ps_out = ctx.enter_context(tc.psum_pool(name="ps_out", bufs=4))
 
-        offs_t = sb.tile([P, S // 16], U16, name="offs_t")
-        left_t = sb.tile([P, V // 16], U16, name="left_t")
-        right_t = sb.tile([P, V // 16], U16, name="right_t")
-        xs_win = sb.tile([P, T], U8, name="xs_win", align_bytes=64)
-        xw_win = sb.tile([P, T], I32, name="xw_win", align_bytes=64)
-        xs_got = sb.tile([P, S], U8, name="xs_got", align_bytes=64)
-        xs_mm = sb.tile([P, S], U8, name="xs_mm", align_bytes=64)
+        offs_list = sb.tile([P, S // LIST], U16, name="offs_list")
+        left_list = sb.tile([P, V // LIST], U16, name="left_list")
+        right_list = sb.tile([P, V // LIST], U16, name="right_list")
+        xs_window = sb.tile([P, T], U8, name="xs_window", tag="scale_window", align_bytes=64)
+        xw_window = sb.tile([P, T], I32, name="xw_window", tag="word_window", align_bytes=64)
+        xs_picked = sb.tile([P, S], U8, name="xs_picked", align_bytes=64)
+        xs_placed = sb.tile([P, S], U8, name="xs_placed", align_bytes=64)
         w2s_raw = sb.tile([P, H], U8, name="w2s_raw", align_bytes=64)
-        w2w_raw = sb.tile([P, 2 * H], U8, name="w2w_raw", align_bytes=64)
 
-        nc.vector.memset(xs_mm[:].bitcast(I32), 0)
+        nc.vector.memset(xs_window[:].bitcast(I32), 0)
+        nc.vector.memset(xs_placed[:].bitcast(I32), 0)
 
-        nc.sync.dma_start(offs_t[:], offs)
-        warm = sb.tile([P, 16], F32, name="warm")
-        nc.vector.memset(warm[:, 0:8], 0.0)
-        nc.scalar.activation(warm[:, 8:16], warm[:, 0:8], ABS)
-        nc.sync.dma_start(
-            xs_win[:].bitcast(I32), x_scales[0].bitcast(I32).unsqueeze(1).to_broadcast([16, 8, T // 4])
-        )
-        nc.sync.dma_start(xw_win[:], x_words[0].rearrange("p n t -> p (n t)").bitcast(I32))
-        nc.sync.dma_start(left_t[:], left)
-        nc.sync.dma_start(right_t[:], right)
         w1_rows = w1.rearrange("(p j) c -> p j c", j=PACK)
-        w1_raw = []
-        for a in range(2):
-            raw = sb.tile([P, PACK, H // 2], F32, name=f"w1_raw{a}", tag=f"w1_raw{a}", align_bytes=64)
-            nc.sync.dma_start(raw[:], w1_rows[:, :, a * (H // 2) : (a + 1) * (H // 2)])
-            w1_raw.append(raw)
-        nc.sync.dma_start(w2w_raw[:].bitcast(I32), w2_words[0].bitcast(I32))
+        w1_cols = [slice(c0, c1) for c0, c1 in zip(W1_CUTS, W1_CUTS[1:])]
+        w1_first = sb.tile([P, PACK, W1_CUTS[1]], F32, name="w1_first")
+        w1_middle = sb.tile([P, PACK, W1_CUTS[2] - W1_CUTS[1]], F32, name="w1_middle")
+        w1_last = sb.tile([P, PACK, H - W1_CUTS[2]], F32, name="w1_last", tag="w1_last", align_bytes=64)
+        nc.sync.dma_start(offs_list[:], offs)
+        nc.sync.dma_start(w1_first[:], w1_rows[:, :, w1_cols[0]])
+        nc.sync.dma_start(xs_window[0:P:8, :].bitcast(I32), x_scales[0].bitcast(I32))
+        nc.sync.dma_start(w1_middle[:], w1_rows[:, :, w1_cols[1]])
+        nc.sync.dma_start(xw_window[:], x_words[0].rearrange("p n t -> p (n t)").bitcast(I32))
+        nc.sync.dma_start(w1_last[:], w1_rows[:, :, w1_cols[2]])
+        nc.sync.dma_start(left_list[:], left)
+        nc.sync.dma_start(right_list[:], right)
         nc.gpsimd.memset(w2s_raw[:].bitcast(I32), 0)
-        for q in range(4):
+        for q in range(QUADRANTS):
             nc.gpsimd.dma_start(
                 w2s_raw[32 * q : 32 * q + 4, :].bitcast(I32), w2_scales[0][4 * q : 4 * q + 4, :].bitcast(I32)
             )
 
-        nc.vector.tensor_copy(xs_got[:], xs_win[:].indirect(offs_t[:]))
-        for q in range(4):
-            nc.scalar.dma_start(
-                xs_mm[32 * q : 32 * q + 4, :].bitcast(I32), xs_got[32 * q : 32 * q + 32 : 8, :].bitcast(I32)
+        nc.vector.tensor_copy(xs_picked[:], xs_window[:].indirect(offs_list[:]))
+        for q in range(QUADRANTS):
+            nc.sync.dma_start(
+                xs_placed[32 * q : 32 * q + 4, :].bitcast(I32), xs_picked[32 * q : 32 * q + 32 : 8, :].bitcast(I32)
             )
-        xw_got = []
-        for a in range(S // BANK):
-            got = sb.tile([P, BANK], I32, name=f"xw_got{a}", align_bytes=64)
-            cols = slice(a * BANK // 16, (a + 1) * BANK // 16)
-            nc.vector.tensor_copy(got[:].bitcast(U32), xw_win[:].bitcast(U32).indirect(offs_t[:, cols]))
-            xw_got.append(got)
+        w2w_raw = sb.tile([P, 2 * H], U8, name="w2w_raw", tag="scale_window", align_bytes=64)
+        nc.sync.dma_start(w2w_raw[:].bitcast(I32), w2_words[0].bitcast(I32))
 
-        w1_b = sb.tile([P, PACK, P, PACK], BF16, name="w1_b", tag="w1_b", align_bytes=64)
-        for a, cast in enumerate((nc.scalar.copy, nc.vector.tensor_copy)):
-            cast(
-                w1_b[:, :, a * 64 : (a + 1) * 64, :].rearrange("p t m j -> p m j t"),
-                w1_raw[a][:].rearrange("p j (m t) -> p m j t", t=PACK),
+        w1_bf = sb.tile([P, PACK, P, PACK], BF16, name="w1_bf", align_bytes=64)
+        for piece, cols in zip((w1_first, w1_middle, w1_last), w1_cols):
+            nc.scalar.copy(
+                w1_bf[:, :, cols.start // PACK : cols.stop // PACK, :].rearrange("p t m j -> p m j t"),
+                piece[:].rearrange("p j (m t) -> p m j t", t=PACK),
             )
-        w1_q = sb.tile([P, H], I32, name="w1_q", align_bytes=64)
-        w1_s = sb.tile([P, H], U8, name="w1_s", align_bytes=64)
-        for t0, t1 in ((0, 1), (1, 2), (2, 4)):
+        w1_codes = sb.tile([P, H], I32, name="w1_codes", align_bytes=64)
+        w1_scale = sb.tile([P, H], U8, name="w1_scale", align_bytes=64)
+
+        def quantise_w1(t0, t1):
             nc.vector.quantize_mx(
-                out=w1_q[:, t0 * P : t1 * P].bitcast(FP8X4),
-                scales=w1_s[:, t0 * P : t1 * P],
-                in_=w1_b[:, t0:t1, :, :].rearrange("p t m j -> p (t m j)"),
+                out=w1_codes[:, t0 * P : t1 * P].bitcast(FP8X4),
+                scales=w1_scale[:, t0 * P : t1 * P],
+                in_=w1_bf[:, t0:t1, :, :].rearrange("p t m j -> p (t m j)"),
             )
 
-        w2_w = sb.tile([P, 2 * H], U8, name="w2_w", tag="w1_b", align_bytes=64)
-        w2_s = sb.tile([P, H], U8, name="w2_s", tag="w1_raw1", align_bytes=64)
+        def gather_words(picked, c0):
+            entries = offs_list[:, c0 // LIST : (c0 + picked.shape[1]) // LIST]
+            nc.vector.tensor_copy(picked[:].bitcast(U32), xw_window[:].bitcast(U32).indirect(entries))
+
+        xw_half = sb.tile([P, 2 * QUARTER], I32, name="xw_half", align_bytes=64)
+        xw_third = sb.tile([P, QUARTER], I32, name="xw_third", align_bytes=64)
+        xw_fourth = sb.tile([P, QUARTER], I32, name="xw_fourth", tag="w1_last", align_bytes=64)
+        gather_words(xw_half, 0)
+        gather_words(xw_third, 2 * QUARTER)
+        quantise_w1(0, 1)
+        gather_words(xw_fourth, 3 * QUARTER)
+        quantise_w1(1, 2)
+        quantise_w1(2, PACK)
+
+        w2_codes = sb.tile([P, 2 * H], U8, name="w2_codes", tag="word_window", align_bytes=64)
+        w2_scale = sb.tile([P, H], U8, name="w2_scale", tag="scale_window", align_bytes=64)
         nc.vector.tensor_copy(
-            w2_w[:].rearrange("p (t m b) -> p t m b", t=PACK, b=2),
+            w2_codes[:].rearrange("p (t m b) -> p t m b", t=PACK, b=2),
             w2w_raw[:].rearrange("p (m t b) -> p t m b", t=PACK, b=2),
         )
         nc.vector.tensor_copy(
-            w2_s[:].rearrange("p (t m) -> p t m", t=PACK), w2s_raw[:].rearrange("p (m t) -> p t m", t=PACK)
+            w2_scale[:].rearrange("p (t m) -> p t m", t=PACK), w2s_raw[:].rearrange("p (m t) -> p t m", t=PACK)
         )
 
-        h = []
-        for t in range(PACK):
-            plane = sb.tile([P, S], F32, name=f"h{t}")
-            for a in range(S // BANK):
-                cols = slice(a * BANK, (a + 1) * BANK)
-                acc = ps_h.tile([P, BANK], F32, name="acc_h")
+        h = [sb.tile([P, S], F32, name=f"h{t}") for t in range(PACK)]
+
+        def project(t, c0, word_tiles, bank):
+            width = sum(words.shape[1] for words in word_tiles)
+            acc = ps_h.tile([P, width], F32, name="acc_h", tag=f"acc_h{bank}")
+            at = 0
+            for words in word_tiles:
                 nc.tensor.matmul_mx(
-                    out=acc[:],
-                    lhsT=w1_q[:, t * P : (t + 1) * P].bitcast(FP8X4),
-                    lhsT_scale=w1_s[:, t * P : (t + 1) * P],
-                    rhs=xw_got[a][:].bitcast(FP8X4),
-                    rhs_scale=xs_mm[:, cols],
+                    out=acc[:, at : at + words.shape[1]],
+                    lhsT=w1_codes[:, t * P : (t + 1) * P].bitcast(FP8X4),
+                    lhsT_scale=w1_scale[:, t * P : (t + 1) * P],
+                    rhs=words.bitcast(FP8X4),
+                    rhs_scale=xs_placed[:, c0 + at : c0 + at + words.shape[1]],
                     start=True,
                     stop=True,
                 )
-                nc.scalar.copy(plane[:, cols], acc[:])
-            h.append(plane)
+                at += words.shape[1]
+            nc.scalar.copy(h[t][:, c0 : c0 + width], acc[:])
 
-        o_q = sb.tile([P, V], I32, name="o_q", align_bytes=64)
-        o_s = sb.tile([P, V], U8, name="o_s", align_bytes=64)
+        quarters = (xw_half[:, 0:QUARTER], xw_half[:, QUARTER : 2 * QUARTER], xw_third[:], xw_fourth[:])
+        for a, words in enumerate(quarters):
+            project(0, a * QUARTER, (words,), a)
+        for t in range(1, PACK):
+            bank = 2 * (t - 1) % H_BANKS
+            project(t, 0, (xw_half[:],), bank)
+            project(t, BANK, quarters[2:], bank + 1)
+
+        groups = V // GROUP
+        diff = [sb.tile([P, PACK, GROUP], F32, name=f"diff{g}") for g in range(groups)]
+        z_tiles = [sb.tile([P, 2 * GROUP], F32, name=f"z_tile{g}", align_bytes=64) for g in range(groups)]
+        fetched = sb.tile([P, 2 * GROUP], F32, name="fetched")
+        out_bf = sb.tile([P, V, PACK], BF16, name="out_bf", align_bytes=64)
+        out_codes = sb.tile([P, V], I32, name="out_codes", align_bytes=64)
+        out_scale = sb.tile([P, V], U8, name="out_scale", align_bytes=64)
         out_rows = out_0.rearrange("(p t) v -> p t v", t=PACK)
         out_words = out_1[0].rearrange("p n t -> p (n t)").bitcast(I32)
+        out_banks = {}
+        out_f32 = {}
 
-        blocks = V // BLOCK
-        diffs = [sb.tile([P, PACK, BLOCK], F32, name=f"diff{b}") for b in range(blocks)]
-        z_in = [sb.tile([P, 2 * BLOCK], F32, name=f"z_in{b}", align_bytes=64) for b in range(blocks)]
-        y_in = [sb.tile([P, 2 * BLOCK], F32, name=f"y_in{b}", align_bytes=64) for b in range(blocks)]
-        spare = [sb.tile([P, 2 * BLOCK], F32, name=f"spare{b}") for b in range(2)]
-        accs = {}
+        def fetch_right(steps, buffer):
+            for e, (g, t) in enumerate(steps):
+                entries = right_list[:, g * GROUP // LIST : (g + 1) * GROUP // LIST]
+                nc.vector.tensor_copy(buffer[:, e * GROUP : (e + 1) * GROUP], h[t][:].indirect(entries))
 
-        def pair_of_units(units, buf, halves=(0, 1)):
-            for (b, t), e in zip(units, halves):
-                cols = slice(b * BLOCK // 16, (b + 1) * BLOCK // 16)
-                nc.vector.tensor_copy(buf[:, e * BLOCK : (e + 1) * BLOCK], h[t][:].indirect(right_t[:, cols]))
-            for (b, t), e in zip(units, halves):
-                cols = slice(b * BLOCK // 16, (b + 1) * BLOCK // 16)
+        def subtract_from_left(steps, buffer, c0, n):
+            for e, (g, t) in enumerate(steps):
+                entries = left_list[:, (g * GROUP + c0) // LIST : (g * GROUP + c0 + n) // LIST]
                 nc.vector.tensor_tensor(
-                    diffs[b][:, t, :], h[t][:].indirect(left_t[:, cols]), buf[:, e * BLOCK : (e + 1) * BLOCK], SUB
+                    diff[g][:, t, c0 : c0 + n],
+                    h[t][:].indirect(entries),
+                    buffer[:, e * GROUP + c0 : e * GROUP + c0 + n],
+                    SUB,
                 )
 
-        def second_layer(b):
-            z_b = z_in[b][:].bitcast(BF16)
+        def differences(steps, buffer):
+            fetch_right(steps, buffer)
+            subtract_from_left(steps, buffer, 0, GROUP)
+
+        def magnitude(g, c0, n):
             nc.scalar.activation(
-                z_b.rearrange("p (c i t) -> p c t i", i=4, t=PACK),
-                diffs[b][:].rearrange("p t (c i) -> p c t i", i=4),
+                z_tiles[g][:, 2 * c0 : 2 * (c0 + n)].bitcast(BF16).rearrange("p (c i t) -> p c t i", i=RUN, t=PACK),
+                diff[g][:, :, c0 : c0 + n].rearrange("p t (c i) -> p c t i", i=RUN),
                 ABS,
             )
-            z_q = sb.tile([P, BLOCK], I32, name=f"z_q{b}", align_bytes=64)
-            z_s = sb.tile([P, BLOCK], U8, name=f"z_s{b}", align_bytes=64)
-            nc.vector.quantize_mx(out=z_q[:].bitcast(FP8X4), scales=z_s[:], in_=z_b)
-            acc = ps_o.tile([P, PACK, BLOCK], F32, name="acc_o")
+
+        def second_product(g, banks):
+            z_codes = sb.tile([P, GROUP], I32, name=f"z_codes{g}", align_bytes=64)
+            z_scale = sb.tile([P, GROUP], U8, name=f"z_scale{g}", align_bytes=64)
+            nc.vector.quantize_mx(out=z_codes[:].bitcast(FP8X4), scales=z_scale[:], in_=z_tiles[g][:].bitcast(BF16))
+            per_bank = PACK // banks
+            out_banks[g] = [ps_out.tile([P, per_bank, GROUP], F32, name="acc_out") for b in range(banks)]
             for t in range(PACK):
                 nc.tensor.matmul_mx(
-                    out=acc[:, t, :],
-                    lhsT=w2_w[:, 2 * t * P : 2 * (t + 1) * P].bitcast(FP4X4),
-                    lhsT_scale=w2_s[:, t * P : (t + 1) * P],
-                    rhs=z_q[:].bitcast(FP8X4),
-                    rhs_scale=z_s[:],
+                    out=out_banks[g][t // per_bank][:, t % per_bank, :],
+                    lhsT=w2_codes[:, 2 * t * P : 2 * (t + 1) * P].bitcast(FP4X4),
+                    lhsT_scale=w2_scale[:, t * P : (t + 1) * P],
+                    rhs=z_codes[:].bitcast(FP8X4),
+                    rhs_scale=z_scale[:],
                     start=True,
                     stop=True,
                 )
-            accs[b] = acc
 
-        def hand_out(b):
-            cols = slice(b * BLOCK, (b + 1) * BLOCK)
-            y = sb.tile([P, PACK, BLOCK], F32, name=f"y{b}")
-            nc.scalar.copy(y[:], accs[b][:])
-            nc.sync.dma_start(out_rows[:, :, cols], y[:])
-            y_b = y_in[b][:].bitcast(BF16)
-            if b < 2:
-                nc.scalar.copy(y_b.rearrange("p (c t) -> p c t", t=PACK), accs[b][:].rearrange("p t c -> p c t"))
-            else:
-                nc.vector.tensor_copy(
-                    y_b.rearrange("p (c i t) -> p c t i", i=4, t=PACK), y[:].rearrange("p t (c i) -> p c t i", i=4)
-                )
-            nc.vector.quantize_mx(out=o_q[:, cols].bitcast(FP8X4), scales=o_s[:, cols], in_=y_b)
+        def store_result(g):
+            result = sb.tile([P, PACK, GROUP], F32, name=f"result{g}")
+            per_bank = PACK // len(out_banks[g])
+            for b, (acc, copy) in enumerate(zip(out_banks[g], (nc.scalar.copy, nc.vector.tensor_copy))):
+                copy(result[:, b * per_bank : (b + 1) * per_bank, :], acc[:])
+            nc.sync.dma_start(out_rows[:, :, g * GROUP : (g + 1) * GROUP], result[:])
+            out_f32[g] = result
 
-        pair_of_units(((0, 0), (1, 0)), spare[0])
-        pair_of_units(((0, 1), (1, 1)), spare[1])
-        pair_of_units(((0, 2), (0, 3)), spare[0])
-        second_layer(0)
-        pair_of_units(((1, 2), (1, 3)), spare[0], (1, 0))
-        second_layer(1)
-        hand_out(0)
-        pair_of_units(((2, 0), (2, 1)), z_in[0])
-        hand_out(1)
-        nc.sync.dma_start(out_words[:, 0 : V // 2], o_q[:, 0 : V // 2])
-        pair_of_units(((2, 2), (2, 3)), z_in[1])
-        second_layer(2)
-        pair_of_units(((3, 0), (3, 1)), y_in[0])
-        pair_of_units(((3, 2), (3, 3)), z_in[2])
-        second_layer(3)
-        hand_out(2)
-        hand_out(3)
-        nc.sync.dma_start(out_words[:, V // 2 : V], o_q[:, V // 2 : V])
+        def round_from_psum(g):
+            nc.scalar.copy(out_bf[:, g * GROUP : (g + 1) * GROUP, :], out_banks[g][0][:].rearrange("p t c -> p c t"))
 
-        for q in range(4):
-            eng = nc.scalar if q % 2 else nc.sync
-            eng.dma_start(out_2[0][4 * q : 4 * q + 4, :].bitcast(I32), o_s[32 * q : 32 * q + 4, :].bitcast(I32))
+        def round_from_sbuf(g):
+            nc.vector.tensor_copy(
+                out_bf[:, g * GROUP : (g + 1) * GROUP, :].rearrange("p (c i) t -> p c t i", i=RUN),
+                out_f32[g][:].rearrange("p t (c i) -> p c t i", i=RUN),
+            )
+
+        def quantise_result(g0, g1):
+            cols = slice(g0 * GROUP, g1 * GROUP)
+            nc.vector.quantize_mx(
+                out=out_codes[:, cols].bitcast(FP8X4),
+                scales=out_scale[:, cols],
+                in_=out_bf[:, cols, :].rearrange("p c t -> p (c t)"),
+            )
+
+        for t in range(PACK):
+            differences(((0, t), (1, t)), fetched)
+        magnitude(0, 0, GROUP)
+        magnitude(1, 0, GROUP)
+        differences(((2, 0), (2, 1)), fetched)
+        second_product(0, 1)
+        differences(((2, 2), (2, 3)), z_tiles[0])
+        magnitude(2, 0, GROUP)
+        second_product(1, 1)
+        store_result(0)
+        round_from_psum(0)
+        differences(((3, 0), (3, 1)), z_tiles[1])
+        second_product(2, 1)
+        store_result(1)
+
+        last_steps = ((3, 2), (3, 3))
+        fetch_right(last_steps, z_tiles[2])
+        for c0 in (0, GROUP // 2):
+            subtract_from_left(last_steps, z_tiles[2], c0, GROUP // 2)
+            magnitude(3, c0, GROUP // 2)
+        round_from_sbuf(1)
+        second_product(3, 2)
+        store_result(2)
+        quantise_result(0, 2)
+        nc.sync.dma_start(out_words[:, 0 : V // 2], out_codes[:, 0 : V // 2])
+        round_from_sbuf(2)
+        store_result(3)
+        round_from_sbuf(3)
+        quantise_result(2, 3)
+        quantise_result(3, 4)
+        nc.sync.dma_start(out_words[:, V // 2 : V], out_codes[:, V // 2 : V])
+
+        for q in range(QUADRANTS):
+            queue = (nc.sync, nc.scalar)[q % 2]
+            queue.dma_start(
+                out_2[0][4 * q : 4 * q + 4, :].bitcast(I32), out_scale[32 * q : 32 * q + 4, :].bitcast(I32)
+            )

@@ -24,8 +24,9 @@ BANK = 512
 H_BANKS = 4
 QUARTER = S // 4
 GROUP = 128
+HALF = GROUP // 2
 RUN = 4
-W1_CUTS = (0, 128, 384, H)
+W1_CUTS = (0, 128, 256, 384, H)
 
 
 def tile_picked_phpair_abs_po_kernel(
@@ -34,8 +35,7 @@ def tile_picked_phpair_abs_po_kernel(
     nc = tc.nc
     with ExitStack() as ctx:
         sb = ctx.enter_context(tc.tile_pool(name="sb", bufs=1))
-        ps_h = ctx.enter_context(tc.psum_pool(name="ps_h", bufs=1))
-        ps_out = ctx.enter_context(tc.psum_pool(name="ps_out", bufs=4))
+        ps = ctx.enter_context(tc.psum_pool(name="ps", bufs=1))
 
         offs_list = sb.tile([P, S // LIST], U16, name="offs_list")
         left_list = sb.tile([P, V // LIST], U16, name="left_list")
@@ -51,15 +51,17 @@ def tile_picked_phpair_abs_po_kernel(
 
         w1_rows = w1.rearrange("(p j) c -> p j c", j=PACK)
         w1_cols = [slice(c0, c1) for c0, c1 in zip(W1_CUTS, W1_CUTS[1:])]
-        w1_first = sb.tile([P, PACK, W1_CUTS[1]], F32, name="w1_first")
-        w1_middle = sb.tile([P, PACK, W1_CUTS[2] - W1_CUTS[1]], F32, name="w1_middle")
-        w1_last = sb.tile([P, PACK, H - W1_CUTS[2]], F32, name="w1_last", tag="w1_last", align_bytes=64)
+        w1_raw = [
+            sb.tile([P, PACK, cols.stop - cols.start], F32, name=f"w1_raw{a}", tag=f"w1_raw{a}", align_bytes=64)
+            for a, cols in enumerate(w1_cols)
+        ]
         nc.sync.dma_start(offs_list[:], offs)
-        nc.sync.dma_start(w1_first[:], w1_rows[:, :, w1_cols[0]])
+        nc.sync.dma_start(w1_raw[0][:], w1_rows[:, :, w1_cols[0]])
         nc.sync.dma_start(xs_window[0:P:8, :].bitcast(I32), x_scales[0].bitcast(I32))
-        nc.sync.dma_start(w1_middle[:], w1_rows[:, :, w1_cols[1]])
+        nc.sync.dma_start(w1_raw[1][:], w1_rows[:, :, w1_cols[1]])
         nc.sync.dma_start(xw_window[:], x_words[0].rearrange("p n t -> p (n t)").bitcast(I32))
-        nc.sync.dma_start(w1_last[:], w1_rows[:, :, w1_cols[2]])
+        nc.sync.dma_start(w1_raw[2][:], w1_rows[:, :, w1_cols[2]])
+        nc.sync.dma_start(w1_raw[3][:], w1_rows[:, :, w1_cols[3]])
         nc.sync.dma_start(left_list[:], left)
         nc.sync.dma_start(right_list[:], right)
         nc.gpsimd.memset(w2s_raw[:].bitcast(I32), 0)
@@ -77,11 +79,17 @@ def tile_picked_phpair_abs_po_kernel(
         nc.sync.dma_start(w2w_raw[:].bitcast(I32), w2_words[0].bitcast(I32))
 
         w1_bf = sb.tile([P, PACK, P, PACK], BF16, name="w1_bf", align_bytes=64)
-        for piece, cols in zip((w1_first, w1_middle, w1_last), w1_cols):
+
+        def round_w1(a, t0, t1):
             nc.scalar.copy(
-                w1_bf[:, :, cols.start // PACK : cols.stop // PACK, :].rearrange("p t m j -> p m j t"),
-                piece[:].rearrange("p j (m t) -> p m j t", t=PACK),
+                w1_bf[:, t0:t1, w1_cols[a].start // PACK : w1_cols[a].stop // PACK, :].rearrange("p t m j -> p m j t"),
+                w1_raw[a][:].rearrange("p j (m t) -> p m j t", t=PACK)[:, :, :, t0:t1],
             )
+
+        for a in range(3):
+            round_w1(a, 0, PACK)
+        round_w1(3, 0, 2)
+        round_w1(3, 2, PACK)
         w1_codes = sb.tile([P, H], I32, name="w1_codes", align_bytes=64)
         w1_scale = sb.tile([P, H], U8, name="w1_scale", align_bytes=64)
 
@@ -98,7 +106,7 @@ def tile_picked_phpair_abs_po_kernel(
 
         xw_half = sb.tile([P, 2 * QUARTER], I32, name="xw_half", align_bytes=64)
         xw_third = sb.tile([P, QUARTER], I32, name="xw_third", align_bytes=64)
-        xw_fourth = sb.tile([P, QUARTER], I32, name="xw_fourth", tag="w1_last", align_bytes=64)
+        xw_fourth = sb.tile([P, QUARTER], I32, name="xw_fourth", tag="w1_raw3", align_bytes=64)
         gather_words(xw_half, 0)
         gather_words(xw_third, 2 * QUARTER)
         quantise_w1(0, 1)
@@ -120,7 +128,7 @@ def tile_picked_phpair_abs_po_kernel(
 
         def project(t, c0, word_tiles, bank):
             width = sum(words.shape[1] for words in word_tiles)
-            acc = ps_h.tile([P, width], F32, name="acc_h", tag=f"acc_h{bank}")
+            acc = ps.tile([P, width], F32, name="acc_h", tag=f"bank{bank}")
             at = 0
             for words in word_tiles:
                 nc.tensor.matmul_mx(
@@ -143,117 +151,143 @@ def tile_picked_phpair_abs_po_kernel(
             project(t, 0, (xw_half[:],), bank)
             project(t, BANK, quarters[2:], bank + 1)
 
-        groups = V // GROUP
-        diff = [sb.tile([P, PACK, GROUP], F32, name=f"diff{g}") for g in range(groups)]
-        z_tiles = [sb.tile([P, 2 * GROUP], F32, name=f"z_tile{g}", align_bytes=64) for g in range(groups)]
-        fetched = sb.tile([P, 2 * GROUP], F32, name="fetched")
-        out_bf = sb.tile([P, V, PACK], BF16, name="out_bf", align_bytes=64)
+        pieces = [(0, GROUP), (GROUP, GROUP), (2 * GROUP, GROUP), (3 * GROUP, HALF), (3 * GROUP + HALF, HALF)]
+        slots = sb.tile([P, 2 * PACK, GROUP], F32, name="slots")
+        diff = [slots[:, 0:4, :], slots[:, 4:8, :], slots[:, 2:6, :], slots[:, 2:6, :]]
+        fetched = sb.tile([P, 2, GROUP], F32, name="fetched", tag="fetched", align_bytes=64)
+        fetched_early = sb.tile([P, 2, GROUP], F32, name="fetched_early")
+        z_bf = [
+            sb.tile([P, n, PACK], BF16, name=f"z_bf{e}", tag=f"z_bf{e}", align_bytes=64)
+            for e, (c0, n) in enumerate(pieces)
+        ]
+        z_codes = sb.tile([P, V], I32, name="z_codes", align_bytes=64)
+        z_scale = sb.tile([P, V], U8, name="z_scale", align_bytes=64)
+        out_bf = {}
         out_codes = sb.tile([P, V], I32, name="out_codes", align_bytes=64)
-        out_scale = sb.tile([P, V], U8, name="out_scale", align_bytes=64)
         out_rows = out_0.rearrange("(p t) v -> p t v", t=PACK)
         out_words = out_1[0].rearrange("p n t -> p (n t)").bitcast(I32)
         out_banks = {}
-        out_f32 = {}
+        results = {}
 
-        def fetch_right(steps, buffer):
-            for e, (g, t) in enumerate(steps):
-                entries = right_list[:, g * GROUP // LIST : (g + 1) * GROUP // LIST]
-                nc.vector.tensor_copy(buffer[:, e * GROUP : (e + 1) * GROUP], h[t][:].indirect(entries))
+        def fetch_right(g, t, buffer):
+            entries = right_list[:, g * GROUP // LIST : (g + 1) * GROUP // LIST]
+            nc.vector.tensor_copy(buffer, h[t][:].indirect(entries))
 
-        def subtract_from_left(steps, buffer, c0, n):
-            for e, (g, t) in enumerate(steps):
-                entries = left_list[:, (g * GROUP + c0) // LIST : (g * GROUP + c0 + n) // LIST]
-                nc.vector.tensor_tensor(
-                    diff[g][:, t, c0 : c0 + n],
-                    h[t][:].indirect(entries),
-                    buffer[:, e * GROUP + c0 : e * GROUP + c0 + n],
-                    SUB,
-                )
+        def subtract_from_left(g, t, buffer, c0=0, n=GROUP):
+            entries = left_list[:, (g * GROUP + c0) // LIST : (g * GROUP + c0 + n) // LIST]
+            nc.vector.tensor_tensor(
+                diff[g][:, t, c0 : c0 + n], h[t][:].indirect(entries), buffer[:, c0 : c0 + n], SUB
+            )
 
-        def differences(steps, buffer):
-            fetch_right(steps, buffer)
-            subtract_from_left(steps, buffer, 0, GROUP)
-
-        def magnitude(g, c0, n):
+        def magnitude(e):
+            c0, n = pieces[e]
             nc.scalar.activation(
-                z_tiles[g][:, 2 * c0 : 2 * (c0 + n)].bitcast(BF16).rearrange("p (c i t) -> p c t i", i=RUN, t=PACK),
-                diff[g][:, :, c0 : c0 + n].rearrange("p t (c i) -> p c t i", i=RUN),
+                z_bf[e][:].rearrange("p (c i) t -> p c t i", i=RUN),
+                diff[c0 // GROUP][:, :, c0 % GROUP : c0 % GROUP + n].rearrange("p t (c i) -> p c t i", i=RUN),
                 ABS,
             )
 
-        def second_product(g, banks):
-            z_codes = sb.tile([P, GROUP], I32, name=f"z_codes{g}", align_bytes=64)
-            z_scale = sb.tile([P, GROUP], U8, name=f"z_scale{g}", align_bytes=64)
-            nc.vector.quantize_mx(out=z_codes[:].bitcast(FP8X4), scales=z_scale[:], in_=z_tiles[g][:].bitcast(BF16))
-            per_bank = PACK // banks
-            out_banks[g] = [ps_out.tile([P, per_bank, GROUP], F32, name="acc_out") for b in range(banks)]
+        def second_product(e):
+            c0, n = pieces[e]
+            nc.vector.quantize_mx(
+                out=z_codes[:, c0 : c0 + n].bitcast(FP8X4),
+                scales=z_scale[:, c0 : c0 + n],
+                in_=z_bf[e][:].rearrange("p c t -> p (c t)"),
+            )
+            moving = slice(c0 + n - GROUP, c0 + n)
+            acc = ps.tile([P, PACK, GROUP], F32, name="acc_out", tag=f"bank{(H_BANKS + e) % (2 * H_BANKS)}")
             for t in range(PACK):
                 nc.tensor.matmul_mx(
-                    out=out_banks[g][t // per_bank][:, t % per_bank, :],
+                    out=acc[:, t, :],
                     lhsT=w2_codes[:, 2 * t * P : 2 * (t + 1) * P].bitcast(FP4X4),
                     lhsT_scale=w2_scale[:, t * P : (t + 1) * P],
-                    rhs=z_codes[:].bitcast(FP8X4),
-                    rhs_scale=z_scale[:],
+                    rhs=z_codes[:, moving].bitcast(FP8X4),
+                    rhs_scale=z_scale[:, moving],
                     start=True,
                     stop=True,
                 )
+            out_banks[e] = acc[:, :, GROUP - n : GROUP]
 
-        def store_result(g):
-            result = sb.tile([P, PACK, GROUP], F32, name=f"result{g}")
-            per_bank = PACK // len(out_banks[g])
-            for b, (acc, copy) in enumerate(zip(out_banks[g], (nc.scalar.copy, nc.vector.tensor_copy))):
-                copy(result[:, b * per_bank : (b + 1) * per_bank, :], acc[:])
-            nc.sync.dma_start(out_rows[:, :, g * GROUP : (g + 1) * GROUP], result[:])
-            out_f32[g] = result
+        def store_result(e, queue):
+            c0, n = pieces[e]
+            result = sb.tile([P, PACK, n], F32, name=f"result{e}")
+            nc.scalar.copy(result[:], out_banks[e])
+            queue.dma_start(out_rows[:, :, c0 : c0 + n], result[:])
+            results[e] = result
 
-        def round_from_psum(g):
-            nc.scalar.copy(out_bf[:, g * GROUP : (g + 1) * GROUP, :], out_banks[g][0][:].rearrange("p t c -> p c t"))
-
-        def round_from_sbuf(g):
+        def round_from_sbuf(e):
+            c0, n = pieces[e]
             nc.vector.tensor_copy(
-                out_bf[:, g * GROUP : (g + 1) * GROUP, :].rearrange("p (c i) t -> p c t i", i=RUN),
-                out_f32[g][:].rearrange("p t (c i) -> p c t i", i=RUN),
+                out_bf[e].rearrange("p (c i) t -> p c t i", i=RUN),
+                results[e][:].rearrange("p t (c i) -> p c t i", i=RUN),
             )
 
-        def quantise_result(g0, g1):
-            cols = slice(g0 * GROUP, g1 * GROUP)
+        def round_result(e, copy):
+            c0, n = pieces[e]
+            copy(out_bf[e], out_banks[e].rearrange("p t c -> p c t"))
+
+        def quantise_result(c0, c1, rounded):
             nc.vector.quantize_mx(
-                out=out_codes[:, cols].bitcast(FP8X4),
-                scales=out_scale[:, cols],
-                in_=out_bf[:, cols, :].rearrange("p c t -> p (c t)"),
+                out=out_codes[:, c0:c1].bitcast(FP8X4),
+                scales=out_scale[:, c0:c1],
+                in_=rounded.rearrange("p c t -> p (c t)"),
             )
+
+        def store_words(c0, c1):
+            nc.sync.dma_start(out_words[:, c0:c1], out_codes[:, c0:c1])
 
         for t in range(PACK):
-            differences(((0, t), (1, t)), fetched)
-        magnitude(0, 0, GROUP)
-        magnitude(1, 0, GROUP)
-        differences(((2, 0), (2, 1)), fetched)
-        second_product(0, 1)
-        differences(((2, 2), (2, 3)), z_tiles[0])
-        magnitude(2, 0, GROUP)
-        second_product(1, 1)
-        store_result(0)
-        round_from_psum(0)
-        differences(((3, 0), (3, 1)), z_tiles[1])
-        second_product(2, 1)
-        store_result(1)
-
-        last_steps = ((3, 2), (3, 3))
-        fetch_right(last_steps, z_tiles[2])
-        for c0 in (0, GROUP // 2):
-            subtract_from_left(last_steps, z_tiles[2], c0, GROUP // 2)
-            magnitude(3, c0, GROUP // 2)
-        round_from_sbuf(1)
-        second_product(3, 2)
-        store_result(2)
-        quantise_result(0, 2)
-        nc.sync.dma_start(out_words[:, 0 : V // 2], out_codes[:, 0 : V // 2])
+            for g in (0, 1):
+                fetch_right(g, t, fetched[:, g, :])
+            for g in (0, 1):
+                subtract_from_left(g, t, fetched[:, g, :])
+        magnitude(0)
+        magnitude(1)
+        buffers = [fetched_early[:, 0, :], fetched_early[:, 1, :], fetched[:, 0, :], fetched[:, 1, :]]
+        for t in range(PACK):
+            fetch_right(2, t, buffers[t])
+        for g in (0, 1):
+            second_product(g)
+            for t in (2 * g, 2 * g + 1):
+                subtract_from_left(2, t, buffers[t])
+        out_early = sb.tile([P, 2 * GROUP, PACK], BF16, name="out_early", align_bytes=64)
+        out_bf[0] = out_early[:, 0:GROUP, :]
+        out_bf[1] = out_early[:, GROUP : 2 * GROUP, :]
+        store_result(0, nc.sync)
+        magnitude(2)
+        round_result(0, nc.scalar.copy)
+        store_result(1, nc.sync)
+        round_result(1, nc.scalar.copy)
+        buffers = [slots[:, 6, :], slots[:, 7, :], fetched[:, 0, :], fetched[:, 1, :]]
+        for t in range(PACK):
+            fetch_right(3, t, buffers[t])
+        second_product(2)
+        for t in range(PACK):
+            subtract_from_left(3, t, buffers[t], 0, HALF)
+        magnitude(3)
+        store_result(2, nc.sync)
+        for t in range(PACK):
+            subtract_from_left(3, t, buffers[t], HALF, HALF)
+        magnitude(4)
+        second_product(3)
+        out_scale = sb.tile([P, V], U8, name="out_scale", tag="z_bf3", align_bytes=64)
+        quantise_result(0, 2 * GROUP, out_early[:])
+        store_words(0, 2 * GROUP)
+        second_product(4)
+        out_late = sb.tile([P, 2 * GROUP, PACK], BF16, name="out_late", tag="z_bf4", align_bytes=64)
+        out_bf[2] = out_late[:, 0:GROUP, :]
+        out_bf[3] = out_late[:, GROUP : GROUP + HALF, :]
+        out_bf[4] = out_late[:, GROUP + HALF : 2 * GROUP, :]
         round_from_sbuf(2)
-        store_result(3)
-        round_from_sbuf(3)
-        quantise_result(2, 3)
-        quantise_result(3, 4)
-        nc.sync.dma_start(out_words[:, V // 2 : V], out_codes[:, V // 2 : V])
+        round_result(3, nc.vector.tensor_copy)
+        store_result(3, nc.sync)
+        quantise_result(2 * GROUP, 3 * GROUP, out_bf[2])
+        store_words(2 * GROUP, 3 * GROUP)
+        round_result(4, nc.vector.tensor_copy)
+        quantise_result(3 * GROUP, 3 * GROUP + HALF, out_bf[3])
+        quantise_result(3 * GROUP + HALF, V, out_bf[4])
+        store_words(3 * GROUP, V)
+        store_result(4, nc.scalar)
 
         for q in range(QUADRANTS):
             queue = (nc.sync, nc.scalar)[q % 2]

@@ -236,11 +236,20 @@ def tile_picked_phpair_abs_po_kernel(
         def store_words(c0, c1):
             nc.sync.dma_start(out_words[:, c0:c1], out_codes[:, c0:c1])
 
-        for t in range(PACK):
-            for g in (0, 1):
-                fetch_right(g, t, fetched[:, g, :])
-            for g in (0, 1):
-                subtract_from_left(g, t, fetched[:, g, :])
+        for t in range(PACK - 1):
+            sides = sb.tile([P, 2, 2 * GROUP], F32, name=f"sides{t}")
+            for side, entries in enumerate((left_list, right_list)):
+                nc.vector.tensor_copy(sides[:, side, :], h[t][:].indirect(entries[:, 0 : 2 * GROUP // LIST]))
+            nc.gpsimd.tensor_tensor(
+                slots[:, t : 2 * PACK : PACK, :],
+                sides[:, 0, :].rearrange("p (g c) -> p g c", g=2),
+                sides[:, 1, :].rearrange("p (g c) -> p g c", g=2),
+                SUB,
+            )
+        for g in (0, 1):
+            fetch_right(g, PACK - 1, fetched[:, g, :])
+        for g in (0, 1):
+            subtract_from_left(g, PACK - 1, fetched[:, g, :])
         magnitude(0)
         magnitude(1)
         buffers = [fetched_early[:, 0, :], fetched_early[:, 1, :], fetched[:, 0, :], fetched[:, 1, :]]

@@ -187,7 +187,7 @@ def tile_picked_phpair_abs_po_kernel(
                 ABS,
             )
 
-        def second_product(e):
+        def second_product(e, banks):
             c0, n = pieces[e]
             nc.vector.quantize_mx(
                 out=z_codes[:, c0 : c0 + n].bitcast(FP8X4),
@@ -195,10 +195,11 @@ def tile_picked_phpair_abs_po_kernel(
                 in_=z_bf[e][:].rearrange("p c t -> p (c t)"),
             )
             moving = slice(c0 + n - GROUP, c0 + n)
-            acc = ps.tile([P, PACK, GROUP], F32, name="acc_out", tag=f"bank{(H_BANKS + e) % (2 * H_BANKS)}")
+            per_bank = PACK // len(banks)
+            accs = [ps.tile([P, per_bank, GROUP], F32, name="acc_out", tag=f"bank{bank}") for bank in banks]
             for t in range(PACK):
                 nc.tensor.matmul_mx(
-                    out=acc[:, t, :],
+                    out=accs[t // per_bank][:, t % per_bank, :],
                     lhsT=w2_codes[:, 2 * t * P : 2 * (t + 1) * P].bitcast(FP4X4),
                     lhsT_scale=w2_scale[:, t * P : (t + 1) * P],
                     rhs=z_codes[:, moving].bitcast(FP8X4),
@@ -206,12 +207,24 @@ def tile_picked_phpair_abs_po_kernel(
                     start=True,
                     stop=True,
                 )
-            out_banks[e] = acc[:, :, GROUP - n : GROUP]
+            out_banks[e] = [acc[:, :, GROUP - n : GROUP] for acc in accs]
+
+        def finish_last(e, queue):
+            c0, n = pieces[e]
+            result = sb.tile([P, PACK, n], F32, name=f"result{e}")
+            per_bank = PACK // len(out_banks[e])
+            for b, acc in enumerate(out_banks[e]):
+                planes = slice(b * per_bank, (b + 1) * per_bank)
+                nc.scalar.copy(out_bf[e][:, :, planes], acc.rearrange("p t c -> p c t"))
+                nc.scalar.copy(result[:, planes, :], acc)
+            queue.dma_start(out_rows[:, :, c0 : c0 + n], result[:])
 
         def store_result(e, queue):
             c0, n = pieces[e]
             result = sb.tile([P, PACK, n], F32, name=f"result{e}")
-            nc.scalar.copy(result[:], out_banks[e])
+            per_bank = PACK // len(out_banks[e])
+            for b, acc in enumerate(out_banks[e]):
+                nc.scalar.copy(result[:, b * per_bank : (b + 1) * per_bank, :], acc)
             queue.dma_start(out_rows[:, :, c0 : c0 + n], result[:])
             results[e] = result
 
@@ -224,7 +237,7 @@ def tile_picked_phpair_abs_po_kernel(
 
         def round_result(e, copy):
             c0, n = pieces[e]
-            copy(out_bf[e], out_banks[e].rearrange("p t c -> p c t"))
+            copy(out_bf[e], out_banks[e][0].rearrange("p t c -> p c t"))
 
         def quantise_result(c0, c1, rounded):
             nc.vector.quantize_mx(
@@ -256,7 +269,7 @@ def tile_picked_phpair_abs_po_kernel(
         for t in range(PACK):
             fetch_right(2, t, buffers[t])
         for g in (0, 1):
-            second_product(g)
+            second_product(g, (H_BANKS + g,))
             for t in (2 * g, 2 * g + 1):
                 subtract_from_left(2, t, buffers[t])
         out_early = sb.tile([P, 2 * GROUP, PACK], BF16, name="out_early", align_bytes=64)
@@ -270,7 +283,7 @@ def tile_picked_phpair_abs_po_kernel(
         buffers = [slots[:, 6, :], slots[:, 7, :], fetched[:, 0, :], fetched[:, 1, :]]
         for t in range(PACK):
             fetch_right(3, t, buffers[t])
-        second_product(2)
+        second_product(2, (H_BANKS + 2,))
         for t in range(PACK):
             subtract_from_left(3, t, buffers[t], 0, HALF)
         magnitude(3)
@@ -278,25 +291,24 @@ def tile_picked_phpair_abs_po_kernel(
         for t in range(PACK):
             subtract_from_left(3, t, buffers[t], HALF, HALF)
         magnitude(4)
-        second_product(3)
+        second_product(3, (H_BANKS + 3,))
         out_scale = sb.tile([P, V], U8, name="out_scale", tag="z_bf3", align_bytes=64)
         quantise_result(0, 2 * GROUP, out_early[:])
         store_words(0, 2 * GROUP)
-        second_product(4)
+        second_product(4, (0, 1))
         out_late = sb.tile([P, 2 * GROUP, PACK], BF16, name="out_late", tag="z_bf4", align_bytes=64)
         out_bf[2] = out_late[:, 0:GROUP, :]
         out_bf[3] = out_late[:, GROUP : GROUP + HALF, :]
         out_bf[4] = out_late[:, GROUP + HALF : 2 * GROUP, :]
         round_from_sbuf(2)
-        round_result(3, nc.vector.tensor_copy)
         store_result(3, nc.sync)
         quantise_result(2 * GROUP, 3 * GROUP, out_bf[2])
         store_words(2 * GROUP, 3 * GROUP)
-        round_result(4, nc.vector.tensor_copy)
+        round_from_sbuf(3)
+        finish_last(4, nc.scalar)
         quantise_result(3 * GROUP, 3 * GROUP + HALF, out_bf[3])
         quantise_result(3 * GROUP + HALF, V, out_bf[4])
         store_words(3 * GROUP, V)
-        store_result(4, nc.scalar)
 
         for q in range(QUADRANTS):
             queue = (nc.sync, nc.scalar)[q % 2]

@@ -35,6 +35,7 @@ def tile_picked_phpair_abs_po_kernel(
     nc = tc.nc
     with ExitStack() as ctx:
         sb = ctx.enter_context(tc.tile_pool(name="sb", bufs=1))
+        turns = ctx.enter_context(tc.tile_pool(name="turns", bufs=1))
         ps = ctx.enter_context(tc.psum_pool(name="ps", bufs=1))
 
         offs_list = sb.tile([P, S // LIST], U16, name="offs_list")
@@ -117,8 +118,8 @@ def tile_picked_phpair_abs_po_kernel(
         w2_codes = sb.tile([P, 2 * H], U8, name="w2_codes", tag="word_window", align_bytes=64)
         w2_scale = sb.tile([P, H], U8, name="w2_scale", tag="scale_window", align_bytes=64)
         nc.vector.tensor_copy(
-            w2_codes[:].rearrange("p (t m b) -> p t m b", t=PACK, b=2),
-            w2w_raw[:].rearrange("p (m t b) -> p t m b", t=PACK, b=2),
+            w2_codes[:].bitcast(U16).rearrange("p (t m) -> p t m", t=PACK),
+            w2w_raw[:].bitcast(U16).rearrange("p (m t) -> p t m", t=PACK),
         )
         nc.vector.tensor_copy(
             w2_scale[:].rearrange("p (t m) -> p t m", t=PACK), w2s_raw[:].rearrange("p (m t) -> p t m", t=PACK)
@@ -152,14 +153,15 @@ def tile_picked_phpair_abs_po_kernel(
             project(t, BANK, quarters[2:], bank + 1)
 
         pieces = [(0, GROUP), (GROUP, GROUP), (2 * GROUP, GROUP), (3 * GROUP, HALF), (3 * GROUP + HALF, HALF)]
-        slots = sb.tile([P, 2 * PACK, GROUP], F32, name="slots")
-        diff = [slots[:, 0:4, :], slots[:, 4:8, :], slots[:, 2:6, :], slots[:, 2:6, :]]
-        fetched = sb.tile([P, 2, GROUP], F32, name="fetched", tag="fetched", align_bytes=64)
-        fetched_early = sb.tile([P, 2, GROUP], F32, name="fetched_early")
+        slots = sb.tile([P, 3 * PACK, GROUP], F32, name="slots")
+        fetched = sb.tile([P, 3, GROUP], F32, name="fetched")
         z_bf = [
             sb.tile([P, n, PACK], BF16, name=f"z_bf{e}", tag=f"z_bf{e}", align_bytes=64)
-            for e, (c0, n) in enumerate(pieces)
+            for e, (c0, n) in enumerate(pieces[:-1])
         ]
+        z_bf.append(turns.tile([P, HALF, PACK], BF16, name="z_bf_last", offset=1024, align_bytes=64))
+        halves = sb.tile([P, 2, PACK, HALF], F32, name="halves", tag="z_bf2", align_bytes=64)
+        diff = [slots[:, 0:4, :], slots[:, 4:8, :], slots[:, 8:12, :], halves[:, 0], halves[:, 1]]
         z_codes = sb.tile([P, V], I32, name="z_codes", align_bytes=64)
         z_scale = sb.tile([P, V], U8, name="z_scale", align_bytes=64)
         out_bf = {}
@@ -176,14 +178,14 @@ def tile_picked_phpair_abs_po_kernel(
         def subtract_from_left(g, t, buffer, c0=0, n=GROUP):
             entries = left_list[:, (g * GROUP + c0) // LIST : (g * GROUP + c0 + n) // LIST]
             nc.vector.tensor_tensor(
-                diff[g][:, t, c0 : c0 + n], h[t][:].indirect(entries), buffer[:, c0 : c0 + n], SUB
+                diff[g + c0 // HALF][:, t, :], h[t][:].indirect(entries), buffer[:, c0 : c0 + n], SUB
             )
 
-        def magnitude(e):
+        def magnitude(e, t0=0, t1=PACK):
             c0, n = pieces[e]
             nc.scalar.activation(
-                z_bf[e][:].rearrange("p (c i) t -> p c t i", i=RUN),
-                diff[c0 // GROUP][:, :, c0 % GROUP : c0 % GROUP + n].rearrange("p t (c i) -> p c t i", i=RUN),
+                z_bf[e][:, :, t0:t1].rearrange("p (c i) t -> p c t i", i=RUN),
+                diff[e][:, t0:t1, :].rearrange("p t (c i) -> p c t i", i=RUN),
                 ABS,
             )
 
@@ -208,16 +210,6 @@ def tile_picked_phpair_abs_po_kernel(
                     stop=True,
                 )
             out_banks[e] = [acc[:, :, GROUP - n : GROUP] for acc in accs]
-
-        def finish_last(e, queue):
-            c0, n = pieces[e]
-            result = sb.tile([P, PACK, n], F32, name=f"result{e}")
-            per_bank = PACK // len(out_banks[e])
-            for b, acc in enumerate(out_banks[e]):
-                planes = slice(b * per_bank, (b + 1) * per_bank)
-                nc.scalar.copy(out_bf[e][:, :, planes], acc.rearrange("p t c -> p c t"))
-                nc.scalar.copy(result[:, planes, :], acc)
-            queue.dma_start(out_rows[:, :, c0 : c0 + n], result[:])
 
         def store_result(e, queue):
             c0, n = pieces[e]
@@ -250,64 +242,59 @@ def tile_picked_phpair_abs_po_kernel(
             nc.sync.dma_start(out_words[:, c0:c1], out_codes[:, c0:c1])
 
         for t in range(PACK - 1):
-            sides = sb.tile([P, 2, 2 * GROUP], F32, name=f"sides{t}")
+            sides = sb.tile([P, 2, 3 * GROUP], F32, name=f"sides{t}")
             for side, entries in enumerate((left_list, right_list)):
-                nc.vector.tensor_copy(sides[:, side, :], h[t][:].indirect(entries[:, 0 : 2 * GROUP // LIST]))
+                nc.vector.tensor_copy(sides[:, side, :], h[t][:].indirect(entries[:, 0 : 3 * GROUP // LIST]))
             nc.gpsimd.tensor_tensor(
-                slots[:, t : 2 * PACK : PACK, :],
-                sides[:, 0, :].rearrange("p (g c) -> p g c", g=2),
-                sides[:, 1, :].rearrange("p (g c) -> p g c", g=2),
+                slots[:, t : 3 * PACK : PACK, :],
+                sides[:, 0, :].rearrange("p (g c) -> p g c", g=3),
+                sides[:, 1, :].rearrange("p (g c) -> p g c", g=3),
                 SUB,
             )
-        for g in (0, 1):
+        for g in range(3):
+            magnitude(g, 0, 2)
+        for g in range(3):
             fetch_right(g, PACK - 1, fetched[:, g, :])
-        for g in (0, 1):
+        for g in range(3):
             subtract_from_left(g, PACK - 1, fetched[:, g, :])
-        magnitude(0)
-        magnitude(1)
-        buffers = [fetched_early[:, 0, :], fetched_early[:, 1, :], fetched[:, 0, :], fetched[:, 1, :]]
-        for t in range(PACK):
-            fetch_right(2, t, buffers[t])
-        for g in (0, 1):
-            second_product(g, (H_BANKS + g,))
-            for t in (2 * g, 2 * g + 1):
-                subtract_from_left(2, t, buffers[t])
-        out_early = sb.tile([P, 2 * GROUP, PACK], BF16, name="out_early", align_bytes=64)
-        out_bf[0] = out_early[:, 0:GROUP, :]
-        out_bf[1] = out_early[:, GROUP : 2 * GROUP, :]
-        store_result(0, nc.sync)
-        magnitude(2)
-        round_result(0, nc.scalar.copy)
-        store_result(1, nc.sync)
-        round_result(1, nc.scalar.copy)
-        buffers = [slots[:, 6, :], slots[:, 7, :], fetched[:, 0, :], fetched[:, 1, :]]
-        for t in range(PACK):
-            fetch_right(3, t, buffers[t])
-        second_product(2, (H_BANKS + 2,))
-        for t in range(PACK):
-            subtract_from_left(3, t, buffers[t], 0, HALF)
-        magnitude(3)
-        store_result(2, nc.sync)
-        for t in range(PACK):
-            subtract_from_left(3, t, buffers[t], HALF, HALF)
-        magnitude(4)
-        second_product(3, (H_BANKS + 3,))
-        out_scale = sb.tile([P, V], U8, name="out_scale", tag="z_bf3", align_bytes=64)
-        quantise_result(0, 2 * GROUP, out_early[:])
-        store_words(0, 2 * GROUP)
+            magnitude(g, 2, PACK)
+        buffers = [fetched[:, 0, :], slots[:, 2, :], slots[:, 6, :], slots[:, 10, :]]
+        fetch_right(3, 0, buffers[0])
+        for g in range(3):
+            second_product(g, ((4, 5), (6,), (7,))[g])
+            fetch_right(3, g + 1, buffers[g + 1])
+        for g in range(3):
+            store_result(g, nc.sync)
+        for e, c0 in ((3, 0), (4, HALF)):
+            for t in range(PACK):
+                subtract_from_left(3, t, buffers[t], c0, HALF)
+            magnitude(e)
+        out_bf[0] = sb.tile([P, GROUP, PACK], BF16, name="rounded0", align_bytes=64)[:]
+        round_from_sbuf(0)
+        second_product(3, (2,))
         second_product(4, (0, 1))
-        out_late = sb.tile([P, 2 * GROUP, PACK], BF16, name="out_late", tag="z_bf4", align_bytes=64)
-        out_bf[2] = out_late[:, 0:GROUP, :]
-        out_bf[3] = out_late[:, GROUP : GROUP + HALF, :]
-        out_bf[4] = out_late[:, GROUP + HALF : 2 * GROUP, :]
+        out_scale = turns.tile([P, V], U8, name="out_scale", offset=768, align_bytes=64)
+        out_bf[1] = sb.tile([P, GROUP, PACK], BF16, name="rounded1", align_bytes=64)[:]
+        out_bf[2] = turns.tile([P, GROUP, PACK], BF16, name="rounded2", offset=1280, align_bytes=64)[:]
+        round_result(1, nc.scalar.copy)
         round_from_sbuf(2)
-        store_result(3, nc.sync)
-        quantise_result(2 * GROUP, 3 * GROUP, out_bf[2])
-        store_words(2 * GROUP, 3 * GROUP)
-        round_from_sbuf(3)
-        finish_last(4, nc.scalar)
-        quantise_result(3 * GROUP, 3 * GROUP + HALF, out_bf[3])
-        quantise_result(3 * GROUP + HALF, V, out_bf[4])
+        for g in range(3):
+            quantise_result(g * GROUP, (g + 1) * GROUP, out_bf[g])
+        store_words(0, 3 * GROUP)
+        out_late = sb.tile([P, GROUP, PACK], BF16, name="out_late", align_bytes=64)
+        result = sb.tile([P, PACK, GROUP], F32, name="result_late")
+        nc.scalar.copy(result[:, :, 0:HALF], out_banks[3][0])
+        nc.vector.tensor_copy(
+            out_late[:, 0:HALF, :].rearrange("p (c i) t -> p c t i", i=RUN),
+            result[:, :, 0:HALF].rearrange("p t (c i) -> p c t i", i=RUN),
+        )
+        for b, acc in enumerate(out_banks[4]):
+            planes = slice(2 * b, 2 * b + 2)
+            nc.scalar.copy(out_late[:, HALF:, planes], acc.rearrange("p t c -> p c t"))
+            nc.scalar.copy(result[:, planes, HALF:], acc)
+            (nc.sync, nc.scalar)[b].dma_start(out_rows[:, planes, 3 * GROUP :], result[:, planes, :])
+        quantise_result(3 * GROUP, 3 * GROUP + HALF, out_late[:, 0:HALF, :])
+        quantise_result(3 * GROUP + HALF, V, out_late[:, HALF:, :])
         store_words(3 * GROUP, V)
 
         for q in range(QUADRANTS):

@@ -65,7 +65,7 @@ def tile_picked_phpair_abs_po_kernel(
         nc.sync.dma_start(w1_raw[3][:], w1_rows[:, :, w1_cols[3]])
         nc.sync.dma_start(left_list[:], left)
         nc.sync.dma_start(right_list[:], right)
-        nc.gpsimd.memset(w2s_raw[:].bitcast(I32), 0)
+        nc.vector.memset(w2s_raw[:].bitcast(I32), 0)
         for q in range(QUADRANTS):
             nc.gpsimd.dma_start(
                 w2s_raw[32 * q : 32 * q + 4, :].bitcast(I32), w2_scales[0][4 * q : 4 * q + 4, :].bitcast(I32)
@@ -154,14 +154,14 @@ def tile_picked_phpair_abs_po_kernel(
 
         pieces = [(0, GROUP), (GROUP, GROUP), (2 * GROUP, GROUP), (3 * GROUP, HALF), (3 * GROUP + HALF, HALF)]
         slots = sb.tile([P, 3 * PACK, GROUP], F32, name="slots")
-        fetched = sb.tile([P, 3, GROUP], F32, name="fetched")
+        fetched = sb.tile([P, 2, GROUP], F32, name="fetched")
         z_bf = [
             sb.tile([P, n, PACK], BF16, name=f"z_bf{e}", tag=f"z_bf{e}", align_bytes=64)
             for e, (c0, n) in enumerate(pieces[:-1])
         ]
         z_bf.append(turns.tile([P, HALF, PACK], BF16, name="z_bf_last", offset=1024, align_bytes=64))
-        halves = sb.tile([P, 2, PACK, HALF], F32, name="halves", tag="z_bf2", align_bytes=64)
-        diff = [slots[:, 0:4, :], slots[:, 4:8, :], slots[:, 8:12, :], halves[:, 0], halves[:, 1]]
+        halves = sb.tile([P, PACK, GROUP], F32, name="halves", tag="z_bf2", align_bytes=64)
+        diff = [slots[:, 0:4, :], slots[:, 4:8, :], slots[:, 8:12, :], halves[:]]
         z_codes = sb.tile([P, V], I32, name="z_codes", align_bytes=64)
         z_scale = sb.tile([P, V], U8, name="z_scale", align_bytes=64)
         out_bf = {}
@@ -178,14 +178,14 @@ def tile_picked_phpair_abs_po_kernel(
         def subtract_from_left(g, t, buffer, c0=0, n=GROUP):
             entries = left_list[:, (g * GROUP + c0) // LIST : (g * GROUP + c0 + n) // LIST]
             nc.vector.tensor_tensor(
-                diff[g + c0 // HALF][:, t, :], h[t][:].indirect(entries), buffer[:, c0 : c0 + n], SUB
+                diff[g][:, t, c0 : c0 + n], h[t][:].indirect(entries), buffer[:, c0 : c0 + n], SUB
             )
 
         def magnitude(e, t0=0, t1=PACK):
             c0, n = pieces[e]
             nc.scalar.activation(
                 z_bf[e][:, :, t0:t1].rearrange("p (c i) t -> p c t i", i=RUN),
-                diff[e][:, t0:t1, :].rearrange("p t (c i) -> p c t i", i=RUN),
+                diff[c0 // GROUP][:, t0:t1, c0 % GROUP : c0 % GROUP + n].rearrange("p t (c i) -> p c t i", i=RUN),
                 ABS,
             )
 
@@ -242,31 +242,38 @@ def tile_picked_phpair_abs_po_kernel(
             nc.sync.dma_start(out_words[:, c0:c1], out_codes[:, c0:c1])
 
         for t in range(PACK - 1):
+            shared = 3 if t < 2 else 2
             sides = sb.tile([P, 2, 3 * GROUP], F32, name=f"sides{t}")
-            for side, entries in enumerate((left_list, right_list)):
-                nc.vector.tensor_copy(sides[:, side, :], h[t][:].indirect(entries[:, 0 : 3 * GROUP // LIST]))
+            nc.vector.tensor_copy(sides[:, 1, :], h[t][:].indirect(right_list[:, 0 : 3 * GROUP // LIST]))
+            nc.vector.tensor_copy(
+                sides[:, 0, 0 : shared * GROUP], h[t][:].indirect(left_list[:, 0 : shared * GROUP // LIST])
+            )
             nc.gpsimd.tensor_tensor(
-                slots[:, t : 3 * PACK : PACK, :],
-                sides[:, 0, :].rearrange("p (g c) -> p g c", g=3),
-                sides[:, 1, :].rearrange("p (g c) -> p g c", g=3),
+                slots[:, t : shared * PACK : PACK, :],
+                sides[:, 0, 0 : shared * GROUP].rearrange("p (g c) -> p g c", g=shared),
+                sides[:, 1, 0 : shared * GROUP].rearrange("p (g c) -> p g c", g=shared),
                 SUB,
             )
-        for g in range(3):
-            magnitude(g, 0, 2)
-        for g in range(3):
+        subtract_from_left(2, 2, sides[:, 1, 2 * GROUP :])
+        for g in range(2):
             fetch_right(g, PACK - 1, fetched[:, g, :])
-        for g in range(3):
+        for g in range(2):
             subtract_from_left(g, PACK - 1, fetched[:, g, :])
-            magnitude(g, 2, PACK)
-        buffers = [fetched[:, 0, :], slots[:, 2, :], slots[:, 6, :], slots[:, 10, :]]
+            magnitude(g)
+        buffers = [fetched[:, 1, :], slots[:, 0, :], slots[:, 4, :], slots[:, 8, :]]
+        fetch_right(2, PACK - 1, fetched[:, 0, :])
         fetch_right(3, 0, buffers[0])
+        subtract_from_left(2, PACK - 1, fetched[:, 0, :])
+        magnitude(2)
         for g in range(3):
             second_product(g, ((4, 5), (6,), (7,))[g])
             fetch_right(3, g + 1, buffers[g + 1])
         for g in range(3):
             store_result(g, nc.sync)
+        for t in (0, 1):
+            subtract_from_left(3, t, buffers[t])
         for e, c0 in ((3, 0), (4, HALF)):
-            for t in range(PACK):
+            for t in (2, 3):
                 subtract_from_left(3, t, buffers[t], c0, HALF)
             magnitude(e)
         out_bf[0] = sb.tile([P, GROUP, PACK], BF16, name="rounded0", align_bytes=64)[:]
@@ -277,10 +284,11 @@ def tile_picked_phpair_abs_po_kernel(
         out_bf[1] = sb.tile([P, GROUP, PACK], BF16, name="rounded1", align_bytes=64)[:]
         out_bf[2] = turns.tile([P, GROUP, PACK], BF16, name="rounded2", offset=1280, align_bytes=64)[:]
         round_result(1, nc.scalar.copy)
+        quantise_result(0, GROUP, out_bf[0])
         round_from_sbuf(2)
-        for g in range(3):
-            quantise_result(g * GROUP, (g + 1) * GROUP, out_bf[g])
-        store_words(0, 3 * GROUP)
+        quantise_result(GROUP, 2 * GROUP, out_bf[1])
+        store_words(0, 2 * GROUP)
+        quantise_result(2 * GROUP, 3 * GROUP, out_bf[2])
         out_late = sb.tile([P, GROUP, PACK], BF16, name="out_late", align_bytes=64)
         result = sb.tile([P, PACK, GROUP], F32, name="result_late")
         nc.scalar.copy(result[:, :, 0:HALF], out_banks[3][0])
@@ -295,7 +303,7 @@ def tile_picked_phpair_abs_po_kernel(
             (nc.sync, nc.scalar)[b].dma_start(out_rows[:, planes, 3 * GROUP :], result[:, planes, :])
         quantise_result(3 * GROUP, 3 * GROUP + HALF, out_late[:, 0:HALF, :])
         quantise_result(3 * GROUP + HALF, V, out_late[:, HALF:, :])
-        store_words(3 * GROUP, V)
+        store_words(2 * GROUP, V)
 
         for q in range(QUADRANTS):
             queue = (nc.sync, nc.scalar)[q % 2]

@@ -26,7 +26,7 @@ QUARTER = S // 4
 GROUP = 128
 HALF = GROUP // 2
 RUN = 4
-W1_CUTS = (0, 128, 256, 384, H)
+W1_CUTS = (0, 128, 256, H)
 
 
 def tile_picked_phpair_abs_po_kernel(
@@ -62,7 +62,6 @@ def tile_picked_phpair_abs_po_kernel(
         nc.sync.dma_start(w1_raw[1][:], w1_rows[:, :, w1_cols[1]])
         nc.sync.dma_start(xw_window[:], x_words[0].rearrange("p n t -> p (n t)").bitcast(I32))
         nc.sync.dma_start(w1_raw[2][:], w1_rows[:, :, w1_cols[2]])
-        nc.sync.dma_start(w1_raw[3][:], w1_rows[:, :, w1_cols[3]])
         nc.sync.dma_start(left_list[:], left)
         nc.sync.dma_start(right_list[:], right)
         nc.vector.memset(w2s_raw[:].bitcast(I32), 0)
@@ -79,26 +78,27 @@ def tile_picked_phpair_abs_po_kernel(
         w2w_raw = sb.tile([P, 2 * H], U8, name="w2w_raw", tag="scale_window", align_bytes=64)
         nc.sync.dma_start(w2w_raw[:].bitcast(I32), w2_words[0].bitcast(I32))
 
-        w1_bf = sb.tile([P, PACK, P, PACK], BF16, name="w1_bf", align_bytes=64)
+        w1_first = sb.tile([P, 1, P, PACK], BF16, name="w1_first", tag="w1_first", align_bytes=64)
+        w1_rest = sb.tile([P, PACK - 1, P, PACK], BF16, name="w1_rest", align_bytes=64)
 
-        def round_w1(a, t0, t1):
+        def round_w1(a, rounded, t0):
             nc.scalar.copy(
-                w1_bf[:, t0:t1, w1_cols[a].start // PACK : w1_cols[a].stop // PACK, :].rearrange("p t m j -> p m j t"),
-                w1_raw[a][:].rearrange("p j (m t) -> p m j t", t=PACK)[:, :, :, t0:t1],
+                rounded[:, :, w1_cols[a].start // PACK : w1_cols[a].stop // PACK, :].rearrange("p t m j -> p m j t"),
+                w1_raw[a][:].rearrange("p j (m t) -> p m j t", t=PACK)[:, :, :, t0 : t0 + rounded.shape[1]],
             )
 
-        for a in range(3):
-            round_w1(a, 0, PACK)
-        round_w1(3, 0, 2)
-        round_w1(3, 2, PACK)
+        for a in range(len(w1_cols)):
+            round_w1(a, w1_first, 0)
+            round_w1(a, w1_rest, 1)
         w1_codes = sb.tile([P, H], I32, name="w1_codes", align_bytes=64)
         w1_scale = sb.tile([P, H], U8, name="w1_scale", align_bytes=64)
 
-        def quantise_w1(t0, t1):
+        def quantise_w1(t0, rounded):
+            cols = slice(t0 * P, (t0 + rounded.shape[1]) * P)
             nc.vector.quantize_mx(
-                out=w1_codes[:, t0 * P : t1 * P].bitcast(FP8X4),
-                scales=w1_scale[:, t0 * P : t1 * P],
-                in_=w1_bf[:, t0:t1, :, :].rearrange("p t m j -> p (t m j)"),
+                out=w1_codes[:, cols].bitcast(FP8X4),
+                scales=w1_scale[:, cols],
+                in_=rounded.rearrange("p t m j -> p (t m j)"),
             )
 
         def gather_words(picked, c0):
@@ -107,13 +107,13 @@ def tile_picked_phpair_abs_po_kernel(
 
         xw_half = sb.tile([P, 2 * QUARTER], I32, name="xw_half", align_bytes=64)
         xw_third = sb.tile([P, QUARTER], I32, name="xw_third", align_bytes=64)
-        xw_fourth = sb.tile([P, QUARTER], I32, name="xw_fourth", tag="w1_raw3", align_bytes=64)
+        xw_fourth = sb.tile([P, QUARTER], I32, name="xw_fourth", tag="w1_first", align_bytes=64)
         gather_words(xw_half, 0)
         gather_words(xw_third, 2 * QUARTER)
-        quantise_w1(0, 1)
+        quantise_w1(0, w1_first[:])
         gather_words(xw_fourth, 3 * QUARTER)
-        quantise_w1(1, 2)
-        quantise_w1(2, PACK)
+        quantise_w1(1, w1_rest[:, 0:1])
+        quantise_w1(2, w1_rest[:, 1:])
 
         w2_codes = sb.tile([P, 2 * H], U8, name="w2_codes", tag="word_window", align_bytes=64)
         w2_scale = sb.tile([P, H], U8, name="w2_scale", tag="scale_window", align_bytes=64)

@@ -25,6 +25,9 @@ H_BANKS = 4
 QUARTER = S // 4
 GROUP = 128
 HALF = GROUP // 2
+EARLY = 3
+PAIR = 2
+OUT_BANKS = ((4, 5), (6,), (7,), (2,), (0, 1))
 RUN = 4
 W1_CUTS = (0, 128, 256, H)
 
@@ -53,7 +56,7 @@ def tile_picked_phpair_abs_po_kernel(
         w1_rows = w1.rearrange("(p j) c -> p j c", j=PACK)
         w1_cols = [slice(c0, c1) for c0, c1 in zip(W1_CUTS, W1_CUTS[1:])]
         w1_raw = [
-            sb.tile([P, PACK, cols.stop - cols.start], F32, name=f"w1_raw{a}", tag=f"w1_raw{a}", align_bytes=64)
+            sb.tile([P, PACK, cols.stop - cols.start], F32, name=f"w1_raw{a}", align_bytes=64)
             for a, cols in enumerate(w1_cols)
         ]
         nc.sync.dma_start(offs_list[:], offs)
@@ -152,23 +155,22 @@ def tile_picked_phpair_abs_po_kernel(
             project(t, 0, (xw_half[:],), bank)
             project(t, BANK, quarters[2:], bank + 1)
 
-        pieces = [(0, GROUP), (GROUP, GROUP), (2 * GROUP, GROUP), (3 * GROUP, HALF), (3 * GROUP + HALF, HALF)]
-        slots = sb.tile([P, 3 * PACK, GROUP], F32, name="slots")
+        pieces = [(g * GROUP, GROUP) for g in range(EARLY)] + [(EARLY * GROUP, HALF), (EARLY * GROUP + HALF, HALF)]
+        slots = sb.tile([P, EARLY * PACK, GROUP], F32, name="slots")
         fetched = sb.tile([P, 2, GROUP], F32, name="fetched")
         z_bf = [
             sb.tile([P, n, PACK], BF16, name=f"z_bf{e}", tag=f"z_bf{e}", align_bytes=64)
             for e, (c0, n) in enumerate(pieces[:-1])
         ]
         z_bf.append(turns.tile([P, HALF, PACK], BF16, name="z_bf_last", offset=1024, align_bytes=64))
-        halves = sb.tile([P, PACK, GROUP], F32, name="halves", tag="z_bf2", align_bytes=64)
-        diff = [slots[:, 0:4, :], slots[:, 4:8, :], slots[:, 8:12, :], halves[:]]
+        last_diff = sb.tile([P, PACK, GROUP], F32, name="last_diff", tag="z_bf2", align_bytes=64)
+        diff = [slots[:, g * PACK : (g + 1) * PACK, :] for g in range(EARLY)] + [last_diff[:]]
         z_codes = sb.tile([P, V], I32, name="z_codes", align_bytes=64)
         z_scale = sb.tile([P, V], U8, name="z_scale", align_bytes=64)
-        out_bf = {}
         out_codes = sb.tile([P, V], I32, name="out_codes", align_bytes=64)
         out_rows = out_0.rearrange("(p t) v -> p t v", t=PACK)
         out_words = out_1[0].rearrange("p n t -> p (n t)").bitcast(I32)
-        out_banks = {}
+        sums = {}
         results = {}
 
         def fetch_right(g, t, buffer):
@@ -189,8 +191,9 @@ def tile_picked_phpair_abs_po_kernel(
                 ABS,
             )
 
-        def second_product(e, banks):
+        def second_product(e):
             c0, n = pieces[e]
+            banks = OUT_BANKS[e]
             nc.vector.quantize_mx(
                 out=z_codes[:, c0 : c0 + n].bitcast(FP8X4),
                 scales=z_scale[:, c0 : c0 + n],
@@ -209,42 +212,36 @@ def tile_picked_phpair_abs_po_kernel(
                     start=True,
                     stop=True,
                 )
-            out_banks[e] = [acc[:, :, GROUP - n : GROUP] for acc in accs]
+            sums[e] = [acc[:, :, GROUP - n : GROUP] for acc in accs]
 
-        def store_result(e, queue):
-            c0, n = pieces[e]
-            result = sb.tile([P, PACK, n], F32, name=f"result{e}")
-            per_bank = PACK // len(out_banks[e])
-            for b, acc in enumerate(out_banks[e]):
-                nc.scalar.copy(result[:, b * per_bank : (b + 1) * per_bank, :], acc)
-            queue.dma_start(out_rows[:, :, c0 : c0 + n], result[:])
-            results[e] = result
+        def store_result(g):
+            results[g] = sb.tile([P, PACK, GROUP], F32, name=f"result{g}")
+            per_bank = PACK // len(sums[g])
+            for b, acc in enumerate(sums[g]):
+                nc.scalar.copy(results[g][:, b * per_bank : (b + 1) * per_bank, :], acc)
+            nc.sync.dma_start(out_rows[:, :, g * GROUP : (g + 1) * GROUP], results[g][:])
 
-        def round_from_sbuf(e):
-            c0, n = pieces[e]
+        def round_from_sbuf(interleaved, planes):
             nc.vector.tensor_copy(
-                out_bf[e].rearrange("p (c i) t -> p c t i", i=RUN),
-                results[e][:].rearrange("p t (c i) -> p c t i", i=RUN),
+                interleaved.rearrange("p (c i) t -> p c t i", i=RUN), planes.rearrange("p t (c i) -> p c t i", i=RUN)
             )
 
-        def round_result(e, copy):
-            c0, n = pieces[e]
-            copy(out_bf[e], out_banks[e][0].rearrange("p t c -> p c t"))
-
-        def quantise_result(c0, c1, rounded):
+        def quantise_result(e, interleaved):
+            c0, c1 = pieces[e][0], pieces[e][0] + pieces[e][1]
             nc.vector.quantize_mx(
                 out=out_codes[:, c0:c1].bitcast(FP8X4),
                 scales=out_scale[:, c0:c1],
-                in_=rounded.rearrange("p c t -> p (c t)"),
+                in_=interleaved.rearrange("p c t -> p (c t)"),
             )
 
         def store_words(c0, c1):
             nc.sync.dma_start(out_words[:, c0:c1], out_codes[:, c0:c1])
 
-        for t in range(PACK - 1):
-            shared = 3 if t < 2 else 2
-            sides = sb.tile([P, 2, 3 * GROUP], F32, name=f"sides{t}")
-            nc.vector.tensor_copy(sides[:, 1, :], h[t][:].indirect(right_list[:, 0 : 3 * GROUP // LIST]))
+        top = PACK - 1
+        for t in range(top):
+            shared = EARLY if t < top - 1 else EARLY - 1
+            sides = sb.tile([P, 2, EARLY * GROUP], F32, name=f"sides{t}")
+            nc.vector.tensor_copy(sides[:, 1, :], h[t][:].indirect(right_list[:, 0 : EARLY * GROUP // LIST]))
             nc.vector.tensor_copy(
                 sides[:, 0, 0 : shared * GROUP], h[t][:].indirect(left_list[:, 0 : shared * GROUP // LIST])
             )
@@ -254,55 +251,62 @@ def tile_picked_phpair_abs_po_kernel(
                 sides[:, 1, 0 : shared * GROUP].rearrange("p (g c) -> p g c", g=shared),
                 SUB,
             )
-        subtract_from_left(2, 2, sides[:, 1, 2 * GROUP :])
+        subtract_from_left(EARLY - 1, top - 1, sides[:, 1, shared * GROUP :])
+        for g in range(EARLY):
+            magnitude(g, 0, PAIR)
+
         for g in range(2):
-            fetch_right(g, PACK - 1, fetched[:, g, :])
+            fetch_right(g, top, fetched[:, g, :])
         for g in range(2):
-            subtract_from_left(g, PACK - 1, fetched[:, g, :])
-            magnitude(g)
-        buffers = [fetched[:, 1, :], slots[:, 0, :], slots[:, 4, :], slots[:, 8, :]]
-        fetch_right(2, PACK - 1, fetched[:, 0, :])
-        fetch_right(3, 0, buffers[0])
-        subtract_from_left(2, PACK - 1, fetched[:, 0, :])
-        magnitude(2)
-        for g in range(3):
-            second_product(g, ((4, 5), (6,), (7,))[g])
-            fetch_right(3, g + 1, buffers[g + 1])
-        for g in range(3):
-            store_result(g, nc.sync)
-        for t in (0, 1):
-            subtract_from_left(3, t, buffers[t])
-        for e, c0 in ((3, 0), (4, HALF)):
-            for t in (2, 3):
-                subtract_from_left(3, t, buffers[t], c0, HALF)
+            subtract_from_left(g, top, fetched[:, g, :])
+            magnitude(g, PAIR, PACK)
+        last_right = [fetched[:, 1, :]] + [diff[g][:, PAIR, :] for g in range(EARLY)]
+        fetch_right(2, top, fetched[:, 0, :])
+        fetch_right(EARLY, 0, last_right[0])
+        subtract_from_left(2, top, fetched[:, 0, :])
+        magnitude(2, PAIR, PACK)
+
+        for g in range(EARLY):
+            second_product(g)
+            fetch_right(EARLY, g + 1, last_right[g + 1])
+        for g in range(EARLY):
+            store_result(g)
+
+        first_half, second_half = EARLY, EARLY + 1
+        for t in range(PAIR):
+            subtract_from_left(EARLY, t, last_right[t])
+        for e, c0 in ((first_half, 0), (second_half, HALF)):
+            for t in range(PAIR, PACK):
+                subtract_from_left(EARLY, t, last_right[t], c0, HALF)
             magnitude(e)
-        out_bf[0] = sb.tile([P, GROUP, PACK], BF16, name="rounded0", align_bytes=64)[:]
-        round_from_sbuf(0)
-        second_product(3, (2,))
-        second_product(4, (0, 1))
+
+        rounded = [
+            sb.tile([P, GROUP, PACK], BF16, name="rounded0", align_bytes=64),
+            sb.tile([P, GROUP, PACK], BF16, name="rounded1", align_bytes=64),
+            turns.tile([P, GROUP, PACK], BF16, name="rounded2", offset=1280, align_bytes=64),
+        ]
+        round_from_sbuf(rounded[0][:], results[0][:])
+        second_product(first_half)
+        second_product(second_half)
         out_scale = turns.tile([P, V], U8, name="out_scale", offset=768, align_bytes=64)
-        out_bf[1] = sb.tile([P, GROUP, PACK], BF16, name="rounded1", align_bytes=64)[:]
-        out_bf[2] = turns.tile([P, GROUP, PACK], BF16, name="rounded2", offset=1280, align_bytes=64)[:]
-        round_result(1, nc.scalar.copy)
-        quantise_result(0, GROUP, out_bf[0])
-        round_from_sbuf(2)
-        quantise_result(GROUP, 2 * GROUP, out_bf[1])
+        nc.scalar.copy(rounded[1][:], sums[1][0].rearrange("p t c -> p c t"))
+        quantise_result(0, rounded[0][:])
+        round_from_sbuf(rounded[2][:], results[2][:])
+        quantise_result(1, rounded[1][:])
         store_words(0, 2 * GROUP)
-        quantise_result(2 * GROUP, 3 * GROUP, out_bf[2])
-        out_late = sb.tile([P, GROUP, PACK], BF16, name="out_late", align_bytes=64)
-        result = sb.tile([P, PACK, GROUP], F32, name="result_late")
-        nc.scalar.copy(result[:, :, 0:HALF], out_banks[3][0])
-        nc.vector.tensor_copy(
-            out_late[:, 0:HALF, :].rearrange("p (c i) t -> p c t i", i=RUN),
-            result[:, :, 0:HALF].rearrange("p t (c i) -> p c t i", i=RUN),
-        )
-        for b, acc in enumerate(out_banks[4]):
-            planes = slice(2 * b, 2 * b + 2)
-            nc.scalar.copy(out_late[:, HALF:, planes], acc.rearrange("p t c -> p c t"))
-            nc.scalar.copy(result[:, planes, HALF:], acc)
-            (nc.sync, nc.scalar)[b].dma_start(out_rows[:, planes, 3 * GROUP :], result[:, planes, :])
-        quantise_result(3 * GROUP, 3 * GROUP + HALF, out_late[:, 0:HALF, :])
-        quantise_result(3 * GROUP + HALF, V, out_late[:, HALF:, :])
+        quantise_result(2, rounded[2][:])
+
+        last_rounded = sb.tile([P, GROUP, PACK], BF16, name="last_rounded", align_bytes=64)
+        last_result = sb.tile([P, PACK, GROUP], F32, name="last_result")
+        nc.scalar.copy(last_result[:, :, 0:HALF], sums[first_half][0])
+        round_from_sbuf(last_rounded[:, 0:HALF, :], last_result[:, :, 0:HALF])
+        for b, acc in enumerate(sums[second_half]):
+            planes = slice(PAIR * b, PAIR * (b + 1))
+            nc.scalar.copy(last_rounded[:, HALF:, planes], acc.rearrange("p t c -> p c t"))
+            nc.scalar.copy(last_result[:, planes, HALF:], acc)
+            (nc.sync, nc.scalar)[b].dma_start(out_rows[:, planes, EARLY * GROUP :], last_result[:, planes, :])
+        quantise_result(first_half, last_rounded[:, 0:HALF, :])
+        quantise_result(second_half, last_rounded[:, HALF:, :])
         store_words(2 * GROUP, V)
 
         for q in range(QUADRANTS):

@@ -29,7 +29,7 @@ EARLY = 3
 PAIR = 2
 OUT_BANKS = ((4, 5), (6,), (7,), (2,), (0, 1))
 RUN = 4
-W1_CUTS = (0, 128, 256, H)
+W1_PIECES = ((0, 2, 0, 256), (0, 2, 256, H), (2, 4, 0, H))
 
 
 def tile_picked_phpair_abs_po_kernel(
@@ -54,17 +54,21 @@ def tile_picked_phpair_abs_po_kernel(
         nc.vector.memset(xs_placed[:].bitcast(I32), 0)
 
         w1_rows = w1.rearrange("(p j) c -> p j c", j=PACK)
-        w1_cols = [slice(c0, c1) for c0, c1 in zip(W1_CUTS, W1_CUTS[1:])]
         w1_raw = [
-            sb.tile([P, PACK, cols.stop - cols.start], F32, name=f"w1_raw{a}", align_bytes=64)
-            for a, cols in enumerate(w1_cols)
+            sb.tile([P, j1 - j0, c1 - c0], F32, name=f"w1_raw{a}", align_bytes=64)
+            for a, (j0, j1, c0, c1) in enumerate(W1_PIECES)
         ]
+
+        def load_w1(a):
+            j0, j1, c0, c1 = W1_PIECES[a]
+            nc.sync.dma_start(w1_raw[a][:], w1_rows[:, j0:j1, c0:c1])
+
+        load_w1(0)
         nc.sync.dma_start(offs_list[:], offs)
-        nc.sync.dma_start(w1_raw[0][:], w1_rows[:, :, w1_cols[0]])
         nc.sync.dma_start(xs_window[0:P:8, :].bitcast(I32), x_scales[0].bitcast(I32))
-        nc.sync.dma_start(w1_raw[1][:], w1_rows[:, :, w1_cols[1]])
+        load_w1(1)
         nc.sync.dma_start(xw_window[:], x_words[0].rearrange("p n t -> p (n t)").bitcast(I32))
-        nc.sync.dma_start(w1_raw[2][:], w1_rows[:, :, w1_cols[2]])
+        load_w1(2)
         nc.sync.dma_start(left_list[:], left)
         nc.sync.dma_start(right_list[:], right)
         nc.vector.memset(w2s_raw[:].bitcast(I32), 0)
@@ -85,12 +89,13 @@ def tile_picked_phpair_abs_po_kernel(
         w1_rest = sb.tile([P, PACK - 1, P, PACK], BF16, name="w1_rest", align_bytes=64)
 
         def round_w1(a, rounded, t0):
+            j0, j1, c0, c1 = W1_PIECES[a]
             nc.scalar.copy(
-                rounded[:, :, w1_cols[a].start // PACK : w1_cols[a].stop // PACK, :].rearrange("p t m j -> p m j t"),
+                rounded[:, :, c0 // PACK : c1 // PACK, j0:j1].rearrange("p t m j -> p m j t"),
                 w1_raw[a][:].rearrange("p j (m t) -> p m j t", t=PACK)[:, :, :, t0 : t0 + rounded.shape[1]],
             )
 
-        for a in range(len(w1_cols)):
+        for a in range(len(W1_PIECES)):
             round_w1(a, w1_first, 0)
             round_w1(a, w1_rest, 1)
         w1_codes = sb.tile([P, H], I32, name="w1_codes", align_bytes=64)

@@ -66,8 +66,8 @@ def tile_picked_phpair_abs_po_kernel(
         load_w1(0)
         nc.sync.dma_start(offs_list[:], offs)
         nc.sync.dma_start(xs_window[0:P:8, :].bitcast(I32), x_scales[0].bitcast(I32))
-        load_w1(1)
         nc.sync.dma_start(xw_window[:], x_words[0].rearrange("p n t -> p (n t)").bitcast(I32))
+        load_w1(1)
         load_w1(2)
         nc.sync.dma_start(left_list[:], left)
         nc.sync.dma_start(right_list[:], right)
@@ -88,16 +88,19 @@ def tile_picked_phpair_abs_po_kernel(
         w1_first = sb.tile([P, 1, P, PACK], BF16, name="w1_first", tag="w1_first", align_bytes=64)
         w1_rest = sb.tile([P, PACK - 1, P, PACK], BF16, name="w1_rest", align_bytes=64)
 
-        def round_w1(a, rounded, t0):
+        def round_w1(copy, a, rounded, t0):
             j0, j1, c0, c1 = W1_PIECES[a]
-            nc.scalar.copy(
+            copy(
                 rounded[:, :, c0 // PACK : c1 // PACK, j0:j1].rearrange("p t m j -> p m j t"),
                 w1_raw[a][:].rearrange("p j (m t) -> p m j t", t=PACK)[:, :, :, t0 : t0 + rounded.shape[1]],
             )
 
-        for a in range(len(W1_PIECES)):
-            round_w1(a, w1_first, 0)
-            round_w1(a, w1_rest, 1)
+        for a in range(2):
+            round_w1(nc.scalar.copy, a, w1_first[:], 0)
+            round_w1(nc.scalar.copy, a, w1_rest[:], 1)
+        round_w1(nc.vector.tensor_copy, 2, w1_first[:], 0)
+        round_w1(nc.vector.tensor_copy, 2, w1_rest[:, 2:3], 3)
+        round_w1(nc.scalar.copy, 2, w1_rest[:, 0:2], 1)
         w1_codes = sb.tile([P, H], I32, name="w1_codes", align_bytes=64)
         w1_scale = sb.tile([P, H], U8, name="w1_scale", align_bytes=64)
 

@@ -14,6 +14,7 @@ U8 = mybir.dt.uint8
 FP8X4 = mybir.dt.float8_e4m3fn_x4
 FP4X4 = mybir.dt.float4_e2m1fn_x4
 ABS = mybir.ActivationFunctionType.Abs
+COPY = mybir.ActivationFunctionType.Copy
 SUB = mybir.AluOpType.subtract
 
 P = 128
@@ -21,13 +22,12 @@ PACK = 4
 QUADRANTS = 4
 LIST = 16
 BANK = 512
-H_BANKS = 4
 QUARTER = S // 4
 GROUP = 128
-HALF = GROUP // 2
-EARLY = 3
+WIDE = 256
 PAIR = 2
-OUT_BANKS = ((4, 5), (6,), (7,), (2,), (0, 1))
+PIECES = ((0, 256), (256, 128), (384, 128))
+OUT_BANKS = ((2, 3), (4,), (6, 7))
 RUN = 4
 W1_PIECES = ((0, 2, 0, 256), (0, 2, 256, H), (2, 4, 0, H))
 
@@ -138,7 +138,7 @@ def tile_picked_phpair_abs_po_kernel(
 
         h = [sb.tile([P, S], F32, name=f"h{t}") for t in range(PACK)]
 
-        def project(t, c0, word_tiles, bank):
+        def project(t, c0, word_tiles, bank, copy):
             width = sum(words.shape[1] for words in word_tiles)
             acc = ps.tile([P, width], F32, name="acc_h", tag=f"bank{bank}")
             at = 0
@@ -153,63 +153,52 @@ def tile_picked_phpair_abs_po_kernel(
                     stop=True,
                 )
                 at += words.shape[1]
-            nc.scalar.copy(h[t][:, c0 : c0 + width], acc[:])
+            copy(h[t][:, c0 : c0 + width], acc[:])
 
         quarters = (xw_half[:, 0:QUARTER], xw_half[:, QUARTER : 2 * QUARTER], xw_third[:], xw_fourth[:])
         for a, words in enumerate(quarters):
-            project(0, a * QUARTER, (words,), a)
+            project(0, a * QUARTER, (words,), a, nc.scalar.copy)
         for t in range(1, PACK):
-            bank = 2 * (t - 1) % H_BANKS
-            project(t, 0, (xw_half[:],), bank)
-            project(t, BANK, quarters[2:], bank + 1)
+            bank = (2 * t + 2) % 8
+            project(t, 0, (xw_half[:],), bank, nc.scalar.copy)
+            project(t, BANK, quarters[2:], bank + 1, nc.scalar.copy)
 
-        pieces = [(g * GROUP, GROUP) for g in range(EARLY)] + [(EARLY * GROUP, HALF), (EARLY * GROUP + HALF, HALF)]
-        slots = sb.tile([P, EARLY * PACK, GROUP], F32, name="slots")
-        fetched = sb.tile([P, 2, GROUP], F32, name="fetched")
-        z_bf = [
-            sb.tile([P, n, PACK], BF16, name=f"z_bf{e}", tag=f"z_bf{e}", align_bytes=64)
-            for e, (c0, n) in enumerate(pieces[:-1])
-        ]
-        z_bf.append(turns.tile([P, HALF, PACK], BF16, name="z_bf_last", offset=1024, align_bytes=64))
-        last_diff = sb.tile([P, PACK, GROUP], F32, name="last_diff", tag="z_bf2", align_bytes=64)
-        diff = [slots[:, g * PACK : (g + 1) * PACK, :] for g in range(EARLY)] + [last_diff[:]]
         z_codes = sb.tile([P, V], I32, name="z_codes", align_bytes=64)
         z_scale = sb.tile([P, V], U8, name="z_scale", align_bytes=64)
         out_codes = sb.tile([P, V], I32, name="out_codes", align_bytes=64)
         out_rows = out_0.rearrange("(p t) v -> p t v", t=PACK)
         out_words = out_1[0].rearrange("p n t -> p (n t)").bitcast(I32)
         sums = {}
-        results = {}
 
-        def fetch_right(g, t, buffer):
-            entries = right_list[:, g * GROUP // LIST : (g + 1) * GROUP // LIST]
-            nc.vector.tensor_copy(buffer, h[t][:].indirect(entries))
+        def entries(side, c0, n):
+            return side[:, c0 // LIST : (c0 + n) // LIST]
 
-        def subtract_from_left(g, t, buffer, c0=0, n=GROUP):
-            entries = left_list[:, (g * GROUP + c0) // LIST : (g * GROUP + c0 + n) // LIST]
-            nc.vector.tensor_tensor(
-                diff[g][:, t, c0 : c0 + n], h[t][:].indirect(entries), buffer[:, c0 : c0 + n], SUB
-            )
+        def fetch_v(buffer, t, side, c0):
+            nc.vector.tensor_copy(buffer, h[t][:].indirect(entries(side, c0, buffer.shape[1])))
 
-        def magnitude(e, t0=0, t1=PACK):
-            c0, n = pieces[e]
+        def fetch_s(buffer, t, side, c0):
+            nc.scalar.activation(buffer, h[t][:].indirect(entries(side, c0, buffer.shape[1])), COPY)
+
+        def fetch_sub(out, t, c0, fetched):
+            nc.vector.tensor_tensor(out, h[t][:].indirect(entries(left_list, c0, out.shape[1])), fetched, SUB)
+
+        def magnitude(z, d):
             nc.scalar.activation(
-                z_bf[e][:, :, t0:t1].rearrange("p (c i) t -> p c t i", i=RUN),
-                diff[c0 // GROUP][:, t0:t1, c0 % GROUP : c0 % GROUP + n].rearrange("p t (c i) -> p c t i", i=RUN),
-                ABS,
+                z.rearrange("p (c i) t -> p c t i", i=RUN), d.rearrange("p t (c i) -> p c t i", i=RUN), ABS
             )
 
-        def second_product(e):
-            c0, n = pieces[e]
+        def second_product(e, z):
+            c0, n = PIECES[e]
             banks = OUT_BANKS[e]
             nc.vector.quantize_mx(
                 out=z_codes[:, c0 : c0 + n].bitcast(FP8X4),
                 scales=z_scale[:, c0 : c0 + n],
-                in_=z_bf[e][:].rearrange("p c t -> p (c t)"),
+                in_=z.rearrange("p c t -> p (c t)"),
             )
-            moving = slice(c0 + n - GROUP, c0 + n)
+            width = max(n, GROUP)
+            moving = slice(c0 + n - width, c0 + n)
             per_bank = PACK // len(banks)
-            accs = [ps.tile([P, per_bank, GROUP], F32, name="acc_out", tag=f"bank{bank}") for bank in banks]
+            accs = [ps.tile([P, per_bank, width], F32, name="acc_out", tag=f"bank{bank}") for bank in banks]
             for t in range(PACK):
                 nc.tensor.matmul_mx(
                     out=accs[t // per_bank][:, t % per_bank, :],
@@ -220,22 +209,15 @@ def tile_picked_phpair_abs_po_kernel(
                     start=True,
                     stop=True,
                 )
-            sums[e] = [acc[:, :, GROUP - n : GROUP] for acc in accs]
-
-        def store_result(g):
-            results[g] = sb.tile([P, PACK, GROUP], F32, name=f"result{g}")
-            per_bank = PACK // len(sums[g])
-            for b, acc in enumerate(sums[g]):
-                nc.scalar.copy(results[g][:, b * per_bank : (b + 1) * per_bank, :], acc)
-            nc.sync.dma_start(out_rows[:, :, g * GROUP : (g + 1) * GROUP], results[g][:])
+            sums[e] = [acc[:, :, width - n : width] for acc in accs]
 
         def round_from_sbuf(interleaved, planes):
             nc.vector.tensor_copy(
                 interleaved.rearrange("p (c i) t -> p c t i", i=RUN), planes.rearrange("p t (c i) -> p c t i", i=RUN)
             )
 
-        def quantise_result(e, interleaved):
-            c0, c1 = pieces[e][0], pieces[e][0] + pieces[e][1]
+        def quantise_result(c0, interleaved):
+            c1 = c0 + interleaved.shape[1]
             nc.vector.quantize_mx(
                 out=out_codes[:, c0:c1].bitcast(FP8X4),
                 scales=out_scale[:, c0:c1],
@@ -246,76 +228,68 @@ def tile_picked_phpair_abs_po_kernel(
             nc.sync.dma_start(out_words[:, c0:c1], out_codes[:, c0:c1])
 
         top = PACK - 1
+        slots = turns.tile([P, 10, GROUP], F32, name="slots", offset=0, align_bytes=64)
+        diff = [slots[:, 2:10:2, :], slots[:, 3:10:2, :], slots[:, 0:4, :], slots[:, 1:8:2, :]]
+        out_scale = turns.tile([P, V], U8, name="out_scale", offset=0, align_bytes=64)
+        sides = [sb.tile([P, 2, WIDE], F32, name=f"sides{t}") for t in range(top)]
+        z_bf = [sb.tile([P, n, PACK], BF16, name=f"z_bf{e}", align_bytes=64) for e, (c0, n) in enumerate(PIECES)]
+        results = [sb.tile([P, PACK, n], F32, name=f"result{e}") for e, (c0, n) in enumerate(PIECES)]
+        rounded = [sb.tile([P, n, PACK], BF16, name=f"rounded{e}", align_bytes=64) for e, (c0, n) in enumerate(PIECES)]
+
+        def wide(row):
+            return slots[:, row : row + 2, :].rearrange("p g c -> p (g c)")
+
+        def store_bank(e, b, copy=nc.scalar.copy, queue=nc.sync):
+            c0, n = PIECES[e]
+            per_bank = PACK // len(sums[e])
+            planes = slice(per_bank * b, per_bank * (b + 1))
+            copy(results[e][:, planes, :], sums[e][b])
+            queue.dma_start(out_rows[:, planes, c0 : c0 + n], results[e][:, planes, :])
+
         for t in range(top):
-            shared = EARLY if t < top - 1 else EARLY - 1
-            sides = sb.tile([P, 2, EARLY * GROUP], F32, name=f"sides{t}")
-            nc.vector.tensor_copy(sides[:, 1, :], h[t][:].indirect(right_list[:, 0 : EARLY * GROUP // LIST]))
-            nc.vector.tensor_copy(
-                sides[:, 0, 0 : shared * GROUP], h[t][:].indirect(left_list[:, 0 : shared * GROUP // LIST])
-            )
-            nc.gpsimd.tensor_tensor(
-                slots[:, t : shared * PACK : PACK, :],
-                sides[:, 0, 0 : shared * GROUP].rearrange("p (g c) -> p g c", g=shared),
-                sides[:, 1, 0 : shared * GROUP].rearrange("p (g c) -> p g c", g=shared),
-                SUB,
-            )
-        subtract_from_left(EARLY - 1, top - 1, sides[:, 1, shared * GROUP :])
-        for g in range(EARLY):
-            magnitude(g, 0, PAIR)
-
+            fetch_v(sides[t][:, 1, :], t, right_list, 0)
+            fetch_v(sides[t][:, 0, :], t, left_list, 0)
+            nc.gpsimd.tensor_tensor(wide(2 + 2 * t), sides[t][:, 0, :], sides[t][:, 1, :], SUB)
+        fetched = sb.tile([P, PACK, WIDE], F32, name="fetched")
+        results[1] = fetched[:, 0:PAIR, :].rearrange("p a (b c) -> p (a b) c", c=GROUP)
+        fetch_s(fetched[:, 0, 0:GROUP], 0, right_list, WIDE)
+        fetch_s(wide(0), top, right_list, 0)
+        for t in (1, 3):
+            fetch_s(fetched[:, t, 0:GROUP], t, right_list, WIDE)
+        fetch_v(fetched[:, 2, :], 2, right_list, WIDE)
+        fetch_v(fetched[:, 3, GROUP:], 3, right_list, WIDE + GROUP)
         for g in range(2):
-            fetch_right(g, top, fetched[:, g, :])
-        for g in range(2):
-            subtract_from_left(g, top, fetched[:, g, :])
-            magnitude(g, PAIR, PACK)
-        last_right = [fetched[:, 1, :]] + [diff[g][:, PAIR, :] for g in range(EARLY)]
-        fetch_right(2, top, fetched[:, 0, :])
-        fetch_right(EARLY, 0, last_right[0])
-        subtract_from_left(2, top, fetched[:, 0, :])
-        magnitude(2, PAIR, PACK)
-
-        for g in range(EARLY):
-            second_product(g)
-            fetch_right(EARLY, g + 1, last_right[g + 1])
-        for g in range(EARLY):
-            store_result(g)
-
-        first_half, second_half = EARLY, EARLY + 1
+            fetch_sub(diff[g][:, top, :], top, g * GROUP, slots[:, g, :])
+            magnitude(z_bf[0][:, g * GROUP : (g + 1) * GROUP, :], diff[g])
+        for t in range(3):
+            fetch_sub(diff[2][:, t, :], t, WIDE, fetched[:, t, 0:GROUP])
+        second_product(0, z_bf[0][:])
+        fetch_sub(diff[2][:, 3, :], 3, WIDE, fetched[:, 3, 0:GROUP])
+        right3 = [fetched[:, 0, 0:GROUP], fetched[:, 1, 0:GROUP], fetched[:, 2, GROUP:], fetched[:, 3, GROUP:]]
         for t in range(PAIR):
-            subtract_from_left(EARLY, t, last_right[t])
-        for e, c0 in ((first_half, 0), (second_half, HALF)):
-            for t in range(PAIR, PACK):
-                subtract_from_left(EARLY, t, last_right[t], c0, HALF)
-            magnitude(e)
-
-        rounded = [
-            sb.tile([P, GROUP, PACK], BF16, name="rounded0", align_bytes=64),
-            sb.tile([P, GROUP, PACK], BF16, name="rounded1", align_bytes=64),
-            turns.tile([P, GROUP, PACK], BF16, name="rounded2", offset=1280, align_bytes=64),
-        ]
+            fetch_s(right3[t], t, right_list, 3 * GROUP)
+        magnitude(z_bf[1][:], diff[2])
+        store_bank(0, 0)
+        for t in (2, 3):
+            fetch_sub(diff[3][:, t, :], t, 3 * GROUP, right3[t])
+        second_product(1, z_bf[1][:])
+        for t in range(PAIR):
+            fetch_sub(diff[3][:, t, :], t, 3 * GROUP, right3[t])
+        store_bank(0, 1)
+        magnitude(z_bf[2][:], diff[3])
         round_from_sbuf(rounded[0][:], results[0][:])
-        second_product(first_half)
-        second_product(second_half)
-        out_scale = turns.tile([P, V], U8, name="out_scale", offset=768, align_bytes=64)
-        nc.scalar.copy(rounded[1][:], sums[1][0].rearrange("p t c -> p c t"))
+        second_product(2, z_bf[2][:])
+        store_bank(1, 0)
         quantise_result(0, rounded[0][:])
-        round_from_sbuf(rounded[2][:], results[2][:])
-        quantise_result(1, rounded[1][:])
-        store_words(0, 2 * GROUP)
-        quantise_result(2, rounded[2][:])
-
-        last_rounded = sb.tile([P, GROUP, PACK], BF16, name="last_rounded", align_bytes=64)
-        last_result = sb.tile([P, PACK, GROUP], F32, name="last_result")
-        nc.scalar.copy(last_result[:, :, 0:HALF], sums[first_half][0])
-        round_from_sbuf(last_rounded[:, 0:HALF, :], last_result[:, :, 0:HALF])
-        for b, acc in enumerate(sums[second_half]):
-            planes = slice(PAIR * b, PAIR * (b + 1))
-            nc.scalar.copy(last_rounded[:, HALF:, planes], acc.rearrange("p t c -> p c t"))
-            nc.scalar.copy(last_result[:, planes, HALF:], acc)
-            (nc.sync, nc.scalar)[b].dma_start(out_rows[:, planes, EARLY * GROUP :], last_result[:, planes, :])
-        quantise_result(first_half, last_rounded[:, 0:HALF, :])
-        quantise_result(second_half, last_rounded[:, HALF:, :])
-        store_words(2 * GROUP, V)
+        store_words(0, WIDE)
+        round_from_sbuf(rounded[1][:], results[1])
+        nc.scalar.copy(rounded[2][:, :, 0:PAIR], sums[2][0].rearrange("p t c -> p c t"))
+        nc.vector.tensor_copy(rounded[2][:, :, PAIR:], sums[2][1].rearrange("p t c -> p c t"))
+        store_bank(2, 0)
+        quantise_result(WIDE, rounded[1][:])
+        quantise_result(WIDE + GROUP, rounded[2][:])
+        store_bank(2, 1, queue=nc.scalar)
+        store_words(WIDE, V)
 
         for q in range(QUADRANTS):
             queue = (nc.sync, nc.scalar)[q % 2]

@@ -27,7 +27,7 @@ GROUP = 128
 WIDE = 256
 PAIR = 2
 PIECES = ((0, 256), (256, 128), (384, 128))
-OUT_BANKS = ((2, 3), (4,), (6, 7))
+OUT_BANKS = ((2, 3), (4,), (5,))
 RUN = 4
 W1_PIECES = ((0, 2, 0, 256), (0, 2, 256, H), (2, 4, 0, H))
 
@@ -38,7 +38,6 @@ def tile_picked_phpair_abs_po_kernel(
     nc = tc.nc
     with ExitStack() as ctx:
         sb = ctx.enter_context(tc.tile_pool(name="sb", bufs=1))
-        turns = ctx.enter_context(tc.tile_pool(name="turns", bufs=1))
         ps = ctx.enter_context(tc.psum_pool(name="ps", bufs=1))
 
         offs_list = sb.tile([P, S // LIST], U16, name="offs_list")
@@ -227,68 +226,77 @@ def tile_picked_phpair_abs_po_kernel(
         def store_words(c0, c1):
             nc.sync.dma_start(out_words[:, c0:c1], out_codes[:, c0:c1])
 
+        out_scale = sb.tile([P, V], U8, name="out_scale", align_bytes=64)
         top = PACK - 1
-        slots = turns.tile([P, 10, GROUP], F32, name="slots", offset=0, align_bytes=64)
-        diff = [slots[:, 2:10:2, :], slots[:, 3:10:2, :], slots[:, 0:4, :], slots[:, 1:8:2, :]]
-        out_scale = turns.tile([P, V], U8, name="out_scale", offset=0, align_bytes=64)
-        sides = [sb.tile([P, 2, WIDE], F32, name=f"sides{t}") for t in range(top)]
+        slots = sb.tile([P, 12, GROUP], F32, name="slots")
+        diff = [slots[:, 2:9:2, :], slots[:, 5:12:2, :], slots[:, 0:4, :], slots[:, 4:8, :]]
+        sides = [sb.tile([P, 2, WIDE], F32, name=f"sides{t}") for t in range(PAIR)]
         z_bf = [sb.tile([P, n, PACK], BF16, name=f"z_bf{e}", align_bytes=64) for e, (c0, n) in enumerate(PIECES)]
-        results = [sb.tile([P, PACK, n], F32, name=f"result{e}") for e, (c0, n) in enumerate(PIECES)]
         rounded = [sb.tile([P, n, PACK], BF16, name=f"rounded{e}", align_bytes=64) for e, (c0, n) in enumerate(PIECES)]
-
-        def wide(row):
-            return slots[:, row : row + 2, :].rearrange("p g c -> p (g c)")
+        results = [
+            [slots[:, r : r + 4, :].rearrange("p (t g) c -> p t (g c)", t=PAIR) for r in (0, 8)],
+            [sb.tile([P, PACK, GROUP], F32, name="result1")[:]],
+            [sb.tile([P, PACK, GROUP], F32, name="result2")[:]],
+        ]
 
         def store_bank(e, b, copy=nc.scalar.copy, queue=nc.sync):
             c0, n = PIECES[e]
             per_bank = PACK // len(sums[e])
-            planes = slice(per_bank * b, per_bank * (b + 1))
-            copy(results[e][:, planes, :], sums[e][b])
-            queue.dma_start(out_rows[:, planes, c0 : c0 + n], results[e][:, planes, :])
+            copy(results[e][b], sums[e][b])
+            queue.dma_start(out_rows[:, per_bank * b : per_bank * (b + 1), c0 : c0 + n], results[e][b])
 
-        for t in range(top):
+        for t in range(PAIR):
             fetch_v(sides[t][:, 1, :], t, right_list, 0)
             fetch_v(sides[t][:, 0, :], t, left_list, 0)
-            nc.gpsimd.tensor_tensor(wide(2 + 2 * t), sides[t][:, 0, :], sides[t][:, 1, :], SUB)
-        fetched = sb.tile([P, PACK, WIDE], F32, name="fetched")
-        results[1] = fetched[:, 0:PAIR, :].rearrange("p a (b c) -> p (a b) c", c=GROUP)
-        fetch_s(fetched[:, 0, 0:GROUP], 0, right_list, WIDE)
-        fetch_s(wide(0), top, right_list, 0)
-        for t in (1, 3):
-            fetch_s(fetched[:, t, 0:GROUP], t, right_list, WIDE)
-        fetch_v(fetched[:, 2, :], 2, right_list, WIDE)
-        fetch_v(fetched[:, 3, GROUP:], 3, right_list, WIDE + GROUP)
+            nc.gpsimd.tensor_tensor(
+                slots[:, 2 + 2 * t : 6 + 2 * t : 3, :],
+                sides[t][:, 0, :].rearrange("p (g c) -> p g c", g=2),
+                sides[t][:, 1, :].rearrange("p (g c) -> p g c", g=2),
+                SUB,
+            )
+        plane2 = sb.tile([P, V], F32, name="plane2")
+        plane3 = sb.tile([P, WIDE], F32, name="plane3")
+        early = sb.tile([P, GROUP], F32, name="early")
+        right_top = [slots[:, 0, :], slots[:, 3, :]]
+        right2 = [early[:], slots[:, 8, :], plane2[:, WIDE : WIDE + GROUP], plane3[:, 0:GROUP]]
+        right3 = [slots[:, 9, :], slots[:, 11, :], plane2[:, WIDE + GROUP :], plane3[:, GROUP:]]
+        for c0 in (0, WIDE):
+            fetch_v(plane2[:, c0 : c0 + WIDE], 2, right_list, c0)
         for g in range(2):
-            fetch_sub(diff[g][:, top, :], top, g * GROUP, slots[:, g, :])
+            fetch_sub(diff[g][:, 2, :], 2, g * GROUP, plane2[:, g * GROUP : (g + 1) * GROUP])
+        fetch_s(right2[0], 0, right_list, WIDE)
+        for g in range(2):
+            fetch_s(right_top[g], top, right_list, g * GROUP)
+        fetch_s(plane3[:], top, right_list, WIDE)
+        for g in range(2):
+            fetch_sub(diff[g][:, top, :], top, g * GROUP, right_top[g])
             magnitude(z_bf[0][:, g * GROUP : (g + 1) * GROUP, :], diff[g])
-        for t in range(3):
-            fetch_sub(diff[2][:, t, :], t, WIDE, fetched[:, t, 0:GROUP])
+        for t in (0, 3, 2):
+            fetch_sub(diff[2][:, t, :], t, WIDE, right2[t])
+        fetch_sub(diff[3][:, 2, :], 2, 3 * GROUP, right3[2])
         second_product(0, z_bf[0][:])
-        fetch_sub(diff[2][:, 3, :], 3, WIDE, fetched[:, 3, 0:GROUP])
-        right3 = [fetched[:, 0, 0:GROUP], fetched[:, 1, 0:GROUP], fetched[:, 2, GROUP:], fetched[:, 3, GROUP:]]
+        fetch_s(right2[1], 1, right_list, WIDE)
         for t in range(PAIR):
             fetch_s(right3[t], t, right_list, 3 * GROUP)
+        fetch_sub(diff[2][:, 1, :], 1, WIDE, right2[1])
         magnitude(z_bf[1][:], diff[2])
-        store_bank(0, 0)
-        for t in (2, 3):
+        for t in (3, 0, 1):
             fetch_sub(diff[3][:, t, :], t, 3 * GROUP, right3[t])
         second_product(1, z_bf[1][:])
-        for t in range(PAIR):
-            fetch_sub(diff[3][:, t, :], t, 3 * GROUP, right3[t])
-        store_bank(0, 1)
         magnitude(z_bf[2][:], diff[3])
-        round_from_sbuf(rounded[0][:], results[0][:])
+        store_bank(0, 0, nc.vector.tensor_copy)
         second_product(2, z_bf[2][:])
+        store_bank(0, 1)
         store_bank(1, 0)
+        store_bank(2, 0)
+        for b in range(2):
+            round_from_sbuf(rounded[0][:, :, PAIR * b : PAIR * (b + 1)], results[0][b])
+        round_from_sbuf(rounded[1][:], results[1][0])
         quantise_result(0, rounded[0][:])
         store_words(0, WIDE)
-        round_from_sbuf(rounded[1][:], results[1])
-        nc.scalar.copy(rounded[2][:, :, 0:PAIR], sums[2][0].rearrange("p t c -> p c t"))
-        nc.vector.tensor_copy(rounded[2][:, :, PAIR:], sums[2][1].rearrange("p t c -> p c t"))
-        store_bank(2, 0)
+        round_from_sbuf(rounded[2][:], results[2][0])
         quantise_result(WIDE, rounded[1][:])
         quantise_result(WIDE + GROUP, rounded[2][:])
-        store_bank(2, 1, queue=nc.scalar)
         store_words(WIDE, V)
 
         for q in range(QUADRANTS):

@@ -27,7 +27,7 @@ GROUP = 128
 WIDE = 256
 PAIR = 2
 PIECES = ((0, 256), (256, 128), (384, 128))
-OUT_BANKS = ((2, 3), (4,), (5,))
+OUT_BANKS = ((2, 3), (4,), (5, 6))
 RUN = 4
 W1_PIECES = ((0, 2, 0, 256), (0, 2, 256, H), (2, 4, 0, H))
 
@@ -38,13 +38,14 @@ def tile_picked_phpair_abs_po_kernel(
     nc = tc.nc
     with ExitStack() as ctx:
         sb = ctx.enter_context(tc.tile_pool(name="sb", bufs=1))
+        turns = ctx.enter_context(tc.tile_pool(name="turns", bufs=1))
         ps = ctx.enter_context(tc.psum_pool(name="ps", bufs=1))
 
         offs_list = sb.tile([P, S // LIST], U16, name="offs_list")
         left_list = sb.tile([P, V // LIST], U16, name="left_list")
         right_list = sb.tile([P, V // LIST], U16, name="right_list")
         xs_window = sb.tile([P, T], U8, name="xs_window", tag="scale_window", align_bytes=64)
-        xw_window = sb.tile([P, T], I32, name="xw_window", tag="word_window", align_bytes=64)
+        xw_window = turns.tile([P, T], I32, name="xw_window", offset=10240, align_bytes=64)
         xs_picked = sb.tile([P, S], U8, name="xs_picked", align_bytes=64)
         xs_placed = sb.tile([P, S], U8, name="xs_placed", align_bytes=64)
         w2s_raw = sb.tile([P, H], U8, name="w2s_raw", align_bytes=64)
@@ -125,8 +126,8 @@ def tile_picked_phpair_abs_po_kernel(
         quantise_w1(1, w1_rest[:, 0:1])
         quantise_w1(2, w1_rest[:, 1:])
 
-        w2_codes = sb.tile([P, 2 * H], U8, name="w2_codes", tag="word_window", align_bytes=64)
-        w2_scale = sb.tile([P, H], U8, name="w2_scale", tag="scale_window", align_bytes=64)
+        w2_codes = turns.tile([P, 2 * H], U8, name="w2_codes", offset=10240, align_bytes=64)
+        w2_scale = turns.tile([P, H], U8, name="w2_scale", offset=11264, align_bytes=64)
         nc.vector.tensor_copy(
             w2_codes[:].bitcast(U16).rearrange("p (t m) -> p t m", t=PACK),
             w2w_raw[:].bitcast(U16).rearrange("p (m t) -> p t m", t=PACK),
@@ -228,73 +229,71 @@ def tile_picked_phpair_abs_po_kernel(
 
         out_scale = sb.tile([P, V], U8, name="out_scale", align_bytes=64)
         top = PACK - 1
-        slots = sb.tile([P, 12, GROUP], F32, name="slots")
-        diff = [slots[:, 2:9:2, :], slots[:, 5:12:2, :], slots[:, 0:4, :], slots[:, 4:8, :]]
-        sides = [sb.tile([P, 2, WIDE], F32, name=f"sides{t}") for t in range(PAIR)]
+        row = GROUP * 4
+
+        def placed(name, shape, dtype, at):
+            return turns.tile(shape, dtype, name=name, offset=at * row, align_bytes=64)
+
+        diff0 = placed("diff0", [P, 5, GROUP], F32, 0)
+        diff1 = placed("diff1", [P, 5, GROUP], F32, 5)
+        top_right = [placed("top_right0", [P, GROUP], F32, 10), sb.tile([P, GROUP], F32, name="top_right1")]
+        rows = placed("rows", [P, 8, GROUP], F32, 10)
+        diff3 = placed("diff3", [P, PACK, GROUP], F32, 5)
+        late = [placed("late0", [P, GROUP], F32, 4), placed("late1", [P, GROUP], F32, 9)]
+        diff = [diff0[:, 0:PACK, :], diff1[:, 0:PACK, :], rows[:, PACK:, :], diff3[:]]
+        first = rows[:].rearrange("p (t g) c -> p t (g c)", t=PACK)
         z_bf = [sb.tile([P, n, PACK], BF16, name=f"z_bf{e}", align_bytes=64) for e, (c0, n) in enumerate(PIECES)]
-        rounded = [sb.tile([P, n, PACK], BF16, name=f"rounded{e}", align_bytes=64) for e, (c0, n) in enumerate(PIECES)]
-        results = [
-            [slots[:, r : r + 4, :].rearrange("p (t g) c -> p t (g c)", t=PAIR) for r in (0, 8)],
-            [sb.tile([P, PACK, GROUP], F32, name="result1")[:]],
-            [sb.tile([P, PACK, GROUP], F32, name="result2")[:]],
+        rounded = [placed("rounded0", [P, WIDE, PACK], BF16, 5)] + [
+            sb.tile([P, GROUP, PACK], BF16, name=f"rounded{e}", align_bytes=64) for e in (1, 2)
         ]
-
-        def store_bank(e, b, copy=nc.scalar.copy, queue=nc.sync):
-            c0, n = PIECES[e]
-            per_bank = PACK // len(sums[e])
-            copy(results[e][b], sums[e][b])
-            queue.dma_start(out_rows[:, per_bank * b : per_bank * (b + 1), c0 : c0 + n], results[e][b])
-
-        for t in range(PAIR):
-            fetch_v(sides[t][:, 1, :], t, right_list, 0)
-            fetch_v(sides[t][:, 0, :], t, left_list, 0)
-            nc.gpsimd.tensor_tensor(
-                slots[:, 2 + 2 * t : 6 + 2 * t : 3, :],
-                sides[t][:, 0, :].rearrange("p (g c) -> p g c", g=2),
-                sides[t][:, 1, :].rearrange("p (g c) -> p g c", g=2),
-                SUB,
-            )
-        plane2 = sb.tile([P, V], F32, name="plane2")
+        middle = sb.tile([P, PACK, GROUP], F32, name="middle")
+        last = sb.tile([P, PACK, GROUP], F32, name="last")
+        right0 = [sb.tile([P, WIDE], F32, name=f"right0_{t}") for t in range(top)]
+        right2 = [sb.tile([P, GROUP], F32, name=f"right2_{t}") for t in range(top)]
         plane3 = sb.tile([P, WIDE], F32, name="plane3")
         early = sb.tile([P, GROUP], F32, name="early")
-        right_top = [slots[:, 0, :], slots[:, 3, :]]
-        right2 = [early[:], slots[:, 8, :], plane2[:, WIDE : WIDE + GROUP], plane3[:, 0:GROUP]]
-        right3 = [slots[:, 9, :], slots[:, 11, :], plane2[:, WIDE + GROUP :], plane3[:, GROUP:]]
-        for c0 in (0, WIDE):
-            fetch_v(plane2[:, c0 : c0 + WIDE], 2, right_list, c0)
+
+        def store_pair(b, copy):
+            planes = slice(PAIR * b, PAIR * (b + 1))
+            copy(first[:, planes, :], sums[0][b])
+            nc.sync.dma_start(out_rows[:, planes, 0:WIDE], first[:, planes, :])
+
+        for t in range(top):
+            fetch_v(right0[t][:], t, right_list, 0)
+            fetch_v(right2[t][:], t, right_list, WIDE)
+            for g in range(2):
+                fetch_sub(diff[g][:, t, :], t, g * GROUP, right0[t][:, g * GROUP : (g + 1) * GROUP])
+        right3 = [early[:], late[1][:], late[0][:], plane3[:, GROUP:]]
+        fetch_s(right3[0], 0, right_list, 3 * GROUP)
         for g in range(2):
-            fetch_sub(diff[g][:, 2, :], 2, g * GROUP, plane2[:, g * GROUP : (g + 1) * GROUP])
-        fetch_s(right2[0], 0, right_list, WIDE)
-        for g in range(2):
-            fetch_s(right_top[g], top, right_list, g * GROUP)
+            fetch_s(top_right[g][:], top, right_list, g * GROUP)
         fetch_s(plane3[:], top, right_list, WIDE)
         for g in range(2):
-            fetch_sub(diff[g][:, top, :], top, g * GROUP, right_top[g])
+            fetch_sub(diff[g][:, top, :], top, g * GROUP, top_right[g][:])
             magnitude(z_bf[0][:, g * GROUP : (g + 1) * GROUP, :], diff[g])
-        for t in (0, 3, 2):
-            fetch_sub(diff[2][:, t, :], t, WIDE, right2[t])
-        fetch_sub(diff[3][:, 2, :], 2, 3 * GROUP, right3[2])
+        for t in range(PACK):
+            fetch_sub(diff[2][:, t, :], t, WIDE, right2[t][:] if t < top else plane3[:, 0:GROUP])
         second_product(0, z_bf[0][:])
-        fetch_s(right2[1], 1, right_list, WIDE)
-        for t in range(PAIR):
+        for t in (2, 1):
             fetch_s(right3[t], t, right_list, 3 * GROUP)
-        fetch_sub(diff[2][:, 1, :], 1, WIDE, right2[1])
         magnitude(z_bf[1][:], diff[2])
-        for t in (3, 0, 1):
+        store_pair(0, nc.scalar.copy)
+        for t in (3, 0, 2, 1):
             fetch_sub(diff[3][:, t, :], t, 3 * GROUP, right3[t])
         second_product(1, z_bf[1][:])
         magnitude(z_bf[2][:], diff[3])
-        store_bank(0, 0, nc.vector.tensor_copy)
+        store_pair(1, nc.vector.tensor_copy)
         second_product(2, z_bf[2][:])
-        store_bank(0, 1)
-        store_bank(1, 0)
-        store_bank(2, 0)
+        nc.scalar.copy(middle[:], sums[1][0])
+        nc.sync.dma_start(out_rows[:, :, WIDE : WIDE + GROUP], middle[:])
         for b in range(2):
-            round_from_sbuf(rounded[0][:, :, PAIR * b : PAIR * (b + 1)], results[0][b])
-        round_from_sbuf(rounded[1][:], results[1][0])
+            nc.scalar.copy(last[:, PAIR * b : PAIR * (b + 1), :], sums[2][b])
+        nc.sync.dma_start(out_rows[:, :, WIDE + GROUP :], last[:])
+        round_from_sbuf(rounded[0][:], first)
+        round_from_sbuf(rounded[1][:], middle[:])
         quantise_result(0, rounded[0][:])
         store_words(0, WIDE)
-        round_from_sbuf(rounded[2][:], results[2][0])
+        round_from_sbuf(rounded[2][:], last[:])
         quantise_result(WIDE, rounded[1][:])
         quantise_result(WIDE + GROUP, rounded[2][:])
         store_words(WIDE, V)

@@ -85,7 +85,9 @@ def tile_picked_phpair_abs_po_kernel(
         w2w_raw = sb.tile([P, 2 * H], U8, name="w2w_raw", tag="scale_window", align_bytes=64)
         nc.sync.dma_start(w2w_raw[:].bitcast(I32), w2_words[0].bitcast(I32))
 
-        w1_first = sb.tile([P, 1, P, PACK], BF16, name="w1_first", tag="w1_first", align_bytes=64)
+        w1_first = [
+            sb.tile([P, 1, P // 2, PACK], BF16, name=f"w1_first{u}", tag=f"w1_first{u}", align_bytes=64) for u in range(2)
+        ]
         w1_rest = sb.tile([P, PACK - 1, P, PACK], BF16, name="w1_rest", align_bytes=64)
 
         def round_w1(copy, a, rounded, t0):
@@ -95,17 +97,25 @@ def tile_picked_phpair_abs_po_kernel(
                 w1_raw[a][:].rearrange("p j (m t) -> p m j t", t=PACK)[:, :, :, t0 : t0 + rounded.shape[1]],
             )
 
+        def round_first(copy, a, u):
+            j0, j1, c0, c1 = W1_PIECES[a]
+            copy(
+                w1_first[u][:, :, :, j0:j1].rearrange("p t m j -> p m j t"),
+                w1_raw[a][:, :, 256 * u - c0 : 256 * (u + 1) - c0].rearrange("p j (m t) -> p m j t", t=PACK)[:, :, :, 0:1],
+            )
+
         for a in range(2):
-            round_w1(nc.scalar.copy, a, w1_first[:], 0)
+            round_first(nc.scalar.copy, a, a)
             round_w1(nc.scalar.copy, a, w1_rest[:], 1)
-        round_w1(nc.vector.tensor_copy, 2, w1_first[:], 0)
-        round_w1(nc.vector.tensor_copy, 2, w1_rest[:, 2:3], 3)
-        round_w1(nc.scalar.copy, 2, w1_rest[:, 0:2], 1)
+        for u in range(2):
+            round_first(nc.vector.tensor_copy, 2, u)
+        round_w1(nc.scalar.copy, 2, w1_rest[:, 0:1], 1)
+        round_w1(nc.scalar.copy, 2, w1_rest[:, 1:3], 2)
         w1_codes = sb.tile([P, H], I32, name="w1_codes", align_bytes=64)
         w1_scale = sb.tile([P, H], U8, name="w1_scale", align_bytes=64)
 
-        def quantise_w1(t0, rounded):
-            cols = slice(t0 * P, (t0 + rounded.shape[1]) * P)
+        def quantise_w1(c0, rounded):
+            cols = slice(c0, c0 + rounded.shape[1] * rounded.shape[2])
             nc.vector.quantize_mx(
                 out=w1_codes[:, cols].bitcast(FP8X4),
                 scales=w1_scale[:, cols],
@@ -118,13 +128,14 @@ def tile_picked_phpair_abs_po_kernel(
 
         xw_half = sb.tile([P, 2 * QUARTER], I32, name="xw_half", align_bytes=64)
         xw_third = sb.tile([P, QUARTER], I32, name="xw_third", align_bytes=64)
-        xw_fourth = sb.tile([P, QUARTER], I32, name="xw_fourth", tag="w1_first", align_bytes=64)
+        xw_fourth = sb.tile([P, QUARTER], I32, name="xw_fourth", tag="w1_first0", align_bytes=64)
         gather_words(xw_half, 0)
         gather_words(xw_third, 2 * QUARTER)
-        quantise_w1(0, w1_first[:])
+        for u in range(2):
+            quantise_w1(u * P // 2, w1_first[u][:])
         gather_words(xw_fourth, 3 * QUARTER)
-        quantise_w1(1, w1_rest[:, 0:1])
-        quantise_w1(2, w1_rest[:, 1:])
+        quantise_w1(P, w1_rest[:, 0:1])
+        quantise_w1(2 * P, w1_rest[:, 1:])
 
         w2_codes = turns.tile([P, 2 * H], U8, name="w2_codes", offset=10240, align_bytes=64)
         w2_scale = turns.tile([P, H], U8, name="w2_scale", offset=11264, align_bytes=64)
@@ -234,24 +245,22 @@ def tile_picked_phpair_abs_po_kernel(
         def placed(name, shape, dtype, at):
             return turns.tile(shape, dtype, name=name, offset=at * row, align_bytes=64)
 
-        diff0 = placed("diff0", [P, 5, GROUP], F32, 0)
-        diff1 = placed("diff1", [P, 5, GROUP], F32, 5)
-        top_right = [placed("top_right0", [P, GROUP], F32, 10), sb.tile([P, GROUP], F32, name="top_right1")]
-        rows = placed("rows", [P, 8, GROUP], F32, 10)
-        diff3 = placed("diff3", [P, PACK, GROUP], F32, 5)
-        late = [placed("late0", [P, GROUP], F32, 4), placed("late1", [P, GROUP], F32, 9)]
+        diff0 = placed("diff0", [P, 7, GROUP], F32, 0)
+        diff1 = placed("diff1", [P, 5, GROUP], F32, 7)
+        top_right = [placed("top_right0", [P, GROUP], F32, 12), sb.tile([P, GROUP], F32, name="top_right1")]
+        rows = placed("rows", [P, 8, GROUP], F32, 12)
+        diff3 = placed("diff3", [P, PACK, GROUP], F32, 7)
+        right3 = [placed(f"right3_{t}", [P, GROUP], F32, at) for t, at in enumerate((4, 11, 5, 6))]
         diff = [diff0[:, 0:PACK, :], diff1[:, 0:PACK, :], rows[:, PACK:, :], diff3[:]]
         first = rows[:].rearrange("p (t g) c -> p t (g c)", t=PACK)
         z_bf = [sb.tile([P, n, PACK], BF16, name=f"z_bf{e}", align_bytes=64) for e, (c0, n) in enumerate(PIECES)]
-        rounded = [placed("rounded0", [P, WIDE, PACK], BF16, 5)] + [
+        rounded = [placed("rounded0", [P, WIDE, PACK], BF16, 7)] + [
             sb.tile([P, GROUP, PACK], BF16, name=f"rounded{e}", align_bytes=64) for e in (1, 2)
         ]
         middle = sb.tile([P, PACK, GROUP], F32, name="middle")
         last = sb.tile([P, PACK, GROUP], F32, name="last")
         right0 = [sb.tile([P, WIDE], F32, name=f"right0_{t}") for t in range(top)]
-        right2 = [sb.tile([P, GROUP], F32, name=f"right2_{t}") for t in range(top)]
-        plane3 = sb.tile([P, WIDE], F32, name="plane3")
-        early = sb.tile([P, GROUP], F32, name="early")
+        right2 = [sb.tile([P, GROUP], F32, name=f"right2_{t}") for t in range(PACK)]
 
         def store_pair(b, copy):
             planes = slice(PAIR * b, PAIR * (b + 1))
@@ -259,27 +268,31 @@ def tile_picked_phpair_abs_po_kernel(
             nc.sync.dma_start(out_rows[:, planes, 0:WIDE], first[:, planes, :])
 
         for t in range(top):
-            fetch_v(right0[t][:], t, right_list, 0)
-            fetch_v(right2[t][:], t, right_list, WIDE)
+            if t < PAIR:
+                fetch_v(right0[t][:], t, right_list, 0)
+                fetch_v(right2[t][:], t, right_list, WIDE)
+            else:
+                for g in range(2):
+                    fetch_v(right0[t][:, g * GROUP : (g + 1) * GROUP], t, right_list, g * GROUP)
             for g in range(2):
                 fetch_sub(diff[g][:, t, :], t, g * GROUP, right0[t][:, g * GROUP : (g + 1) * GROUP])
-        right3 = [early[:], late[1][:], late[0][:], plane3[:, GROUP:]]
-        fetch_s(right3[0], 0, right_list, 3 * GROUP)
+        fetch_s(right2[2][:], 2, right_list, WIDE)
         for g in range(2):
             fetch_s(top_right[g][:], top, right_list, g * GROUP)
-        fetch_s(plane3[:], top, right_list, WIDE)
+        fetch_s(right2[top][:], top, right_list, WIDE)
         for g in range(2):
             fetch_sub(diff[g][:, top, :], top, g * GROUP, top_right[g][:])
             magnitude(z_bf[0][:, g * GROUP : (g + 1) * GROUP, :], diff[g])
         for t in range(PACK):
-            fetch_sub(diff[2][:, t, :], t, WIDE, right2[t][:] if t < top else plane3[:, 0:GROUP])
+            fetch_sub(diff[2][:, t, :], t, WIDE, right2[t][:])
+        fetch_v(right3[top][:], top, right_list, 3 * GROUP)
         second_product(0, z_bf[0][:])
-        for t in (2, 1):
-            fetch_s(right3[t], t, right_list, 3 * GROUP)
+        for t in (0, 2, 1):
+            fetch_s(right3[t][:], t, right_list, 3 * GROUP)
         magnitude(z_bf[1][:], diff[2])
         store_pair(0, nc.scalar.copy)
         for t in (3, 0, 2, 1):
-            fetch_sub(diff[3][:, t, :], t, 3 * GROUP, right3[t])
+            fetch_sub(diff[3][:, t, :], t, 3 * GROUP, right3[t][:])
         second_product(1, z_bf[1][:])
         magnitude(z_bf[2][:], diff[3])
         store_pair(1, nc.vector.tensor_copy)

@@ -245,16 +245,16 @@ def tile_picked_phpair_abs_po_kernel(
         def placed(name, shape, dtype, at):
             return turns.tile(shape, dtype, name=name, offset=at * row, align_bytes=64)
 
-        diff0 = placed("diff0", [P, 7, GROUP], F32, 0)
-        diff1 = placed("diff1", [P, 5, GROUP], F32, 7)
+        diff0 = placed("diff0", [P, PACK, GROUP], F32, 0)
+        diff1 = placed("diff1", [P, PACK, GROUP], F32, 4)
         top_right = [placed("top_right0", [P, GROUP], F32, 12), sb.tile([P, GROUP], F32, name="top_right1")]
-        rows = placed("rows", [P, 8, GROUP], F32, 12)
-        diff3 = placed("diff3", [P, PACK, GROUP], F32, 7)
-        right3 = [placed(f"right3_{t}", [P, GROUP], F32, at) for t, at in enumerate((4, 11, 5, 6))]
-        diff = [diff0[:, 0:PACK, :], diff1[:, 0:PACK, :], rows[:, PACK:, :], diff3[:]]
+        rows = placed("rows", [P, 8, GROUP], F32, 8)
+        diff3 = placed("diff3", [P, PACK, GROUP], F32, 4)
+        right3 = [placed(f"right3_{t}", [P, GROUP], F32, t) for t in range(PACK)]
+        diff = [diff0[:], diff1[:], rows[:, PACK:, :], diff3[:]]
         first = rows[:].rearrange("p (t g) c -> p t (g c)", t=PACK)
         z_bf = [sb.tile([P, n, PACK], BF16, name=f"z_bf{e}", align_bytes=64) for e, (c0, n) in enumerate(PIECES)]
-        rounded = [placed("rounded0", [P, WIDE, PACK], BF16, 7)] + [
+        rounded = [placed("rounded0", [P, WIDE, PACK], BF16, 4)] + [
             sb.tile([P, GROUP, PACK], BF16, name=f"rounded{e}", align_bytes=64) for e in (1, 2)
         ]
         middle = sb.tile([P, PACK, GROUP], F32, name="middle")

from contextlib import ExitStack

import concourse.mybir as mybir

K, T, S, H, V = 512, 2048, 1024, 512, 512
FLOPS = 2 * K * H * S + 2 * H * H * V

F32 = mybir.dt.float32
BF16 = mybir.dt.bfloat16
I32 = mybir.dt.int32
U32 = mybir.dt.uint32
U16 = mybir.dt.uint16
U8 = mybir.dt.uint8
FP8X4 = mybir.dt.float8_e4m3fn_x4
FP4X4 = mybir.dt.float4_e2m1fn_x4
ABS = mybir.ActivationFunctionType.Abs
COPY = mybir.ActivationFunctionType.Copy
SUB = mybir.AluOpType.subtract

P = 128
PACK = 4
QUADRANTS = 4
LIST = 16
BANK = 512
QUARTER = S // 4
GROUP = 128
WIDE = 256
PAIR = 2
PIECES = ((0, 256), (256, 128), (384, 128))
OUT_BANKS = ((2, 3), (4,), (5, 6))
RUN = 4
W1_PIECES = ((0, 2, 0, 256), (0, 2, 256, H), (2, 4, 0, H))


def tile_picked_phpair_abs_po_kernel(
    tc, x_words, x_scales, w1, w2_words, w2_scales, offs, left, right, out_0, out_1, out_2
):
    nc = tc.nc
    with ExitStack() as ctx:
        sb = ctx.enter_context(tc.tile_pool(name="sb", bufs=1))
        turns = ctx.enter_context(tc.tile_pool(name="turns", bufs=1))
        ps = ctx.enter_context(tc.psum_pool(name="ps", bufs=1))

        offs_list = sb.tile([P, S // LIST], U16, name="offs_list")
        left_list = sb.tile([P, V // LIST], U16, name="left_list")
        right_list = sb.tile([P, V // LIST], U16, name="right_list")
        xs_window = sb.tile([P, T], U8, name="xs_window", tag="scale_window", align_bytes=64)
        xw_window = turns.tile([P, T], I32, name="xw_window", offset=10240, align_bytes=64)
        xs_picked = sb.tile([P, S], U8, name="xs_picked", align_bytes=64)
        xs_placed = sb.tile([P, S], U8, name="xs_placed", align_bytes=64)
        w2s_raw = sb.tile([P, H], U8, name="w2s_raw", align_bytes=64)

        nc.vector.memset(xs_window[:].bitcast(I32), 0)
        nc.vector.memset(xs_placed[:].bitcast(I32), 0)

        w1_rows = w1.rearrange("(p j) c -> p j c", j=PACK)
        w1_raw = [
            sb.tile([P, j1 - j0, c1 - c0], F32, name=f"w1_raw{a}", align_bytes=64)
            for a, (j0, j1, c0, c1) in enumerate(W1_PIECES)
        ]

        def load_w1(a):
            j0, j1, c0, c1 = W1_PIECES[a]
            nc.sync.dma_start(w1_raw[a][:], w1_rows[:, j0:j1, c0:c1])

        load_w1(0)
        nc.sync.dma_start(offs_list[:], offs)
        nc.sync.dma_start(xs_window[0:P:8, :].bitcast(I32), x_scales[0].bitcast(I32))
        nc.sync.dma_start(xw_window[:], x_words[0].rearrange("p n t -> p (n t)").bitcast(I32))
        load_w1(1)
        load_w1(2)
        nc.sync.dma_start(left_list[:], left)
        nc.sync.dma_start(right_list[:], right)
        nc.vector.memset(w2s_raw[:].bitcast(I32), 0)
        for q in range(QUADRANTS):
            nc.gpsimd.dma_start(
                w2s_raw[32 * q : 32 * q + 4, :].bitcast(I32), w2_scales[0][4 * q : 4 * q + 4, :].bitcast(I32)
            )

        nc.vector.tensor_copy(xs_picked[:], xs_window[:].indirect(offs_list[:]))
        for q in range(QUADRANTS):
            nc.sync.dma_start(
                xs_placed[32 * q : 32 * q + 4, :].bitcast(I32), xs_picked[32 * q : 32 * q + 32 : 8, :].bitcast(I32)
            )
        w2w_raw = sb.tile([P, 2 * H], U8, name="w2w_raw", tag="scale_window", align_bytes=64)
        nc.sync.dma_start(w2w_raw[:].bitcast(I32), w2_words[0].bitcast(I32))

        w1_first = [
            sb.tile([P, 1, P // 2, PACK], BF16, name=f"w1_first{u}", tag=f"w1_first{u}", align_bytes=64) for u in range(2)
        ]
        w1_rest = sb.tile([P, PACK - 1, P, PACK], BF16, name="w1_rest", align_bytes=64)

        def round_w1(copy, a, rounded, t0):
            j0, j1, c0, c1 = W1_PIECES[a]
            copy(
                rounded[:, :, c0 // PACK : c1 // PACK, j0:j1].rearrange("p t m j -> p m j t"),
                w1_raw[a][:].rearrange("p j (m t) -> p m j t", t=PACK)[:, :, :, t0 : t0 + rounded.shape[1]],
            )

        def round_first(copy, a, u):
            j0, j1, c0, c1 = W1_PIECES[a]
            copy(
                w1_first[u][:, :, :, j0:j1].rearrange("p t m j -> p m j t"),
                w1_raw[a][:, :, 256 * u - c0 : 256 * (u + 1) - c0].rearrange("p j (m t) -> p m j t", t=PACK)[:, :, :, 0:1],
            )

        for a in range(2):
            round_first(nc.scalar.copy, a, a)
            round_w1(nc.scalar.copy, a, w1_rest[:], 1)
        for u in range(2):
            round_first(nc.vector.tensor_copy, 2, u)
        round_w1(nc.scalar.copy, 2, w1_rest[:, 0:1], 1)
        round_w1(nc.scalar.copy, 2, w1_rest[:, 1:3], 2)
        w1_codes = sb.tile([P, H], I32, name="w1_codes", align_bytes=64)
        w1_scale = sb.tile([P, H], U8, name="w1_scale", align_bytes=64)

        def quantise_w1(c0, rounded):
            cols = slice(c0, c0 + rounded.shape[1] * rounded.shape[2])
            nc.vector.quantize_mx(
                out=w1_codes[:, cols].bitcast(FP8X4),
                scales=w1_scale[:, cols],
                in_=rounded.rearrange("p t m j -> p (t m j)"),
            )

        def gather_words(picked, c0):
            entries = offs_list[:, c0 // LIST : (c0 + picked.shape[1]) // LIST]
            nc.vector.tensor_copy(picked[:].bitcast(U32), xw_window[:].bitcast(U32).indirect(entries))

        xw_half = sb.tile([P, 2 * QUARTER], I32, name="xw_half", align_bytes=64)
        xw_third = sb.tile([P, QUARTER], I32, name="xw_third", align_bytes=64)
        xw_fourth = sb.tile([P, QUARTER], I32, name="xw_fourth", tag="w1_first0", align_bytes=64)
        gather_words(xw_half, 0)
        gather_words(xw_third, 2 * QUARTER)
        for u in range(2):
            quantise_w1(u * P // 2, w1_first[u][:])
        gather_words(xw_fourth, 3 * QUARTER)
        quantise_w1(P, w1_rest[:, 0:1])
        quantise_w1(2 * P, w1_rest[:, 1:])

        w2_codes = turns.tile([P, 2 * H], U8, name="w2_codes", offset=10240, align_bytes=64)
        w2_scale = turns.tile([P, H], U8, name="w2_scale", offset=11264, align_bytes=64)
        nc.vector.tensor_copy(
            w2_codes[:].bitcast(U16).rearrange("p (t m) -> p t m", t=PACK),
            w2w_raw[:].bitcast(U16).rearrange("p (m t) -> p t m", t=PACK),
        )
        nc.vector.tensor_copy(
            w2_scale[:].rearrange("p (t m) -> p t m", t=PACK), w2s_raw[:].rearrange("p (m t) -> p t m", t=PACK)
        )

        h = [sb.tile([P, S], F32, name=f"h{t}") for t in range(PACK)]

        def project(t, c0, word_tiles, bank, copy):
            width = sum(words.shape[1] for words in word_tiles)
            acc = ps.tile([P, width], F32, name="acc_h", tag=f"bank{bank}")
            at = 0
            for words in word_tiles:
                nc.tensor.matmul_mx(
                    out=acc[:, at : at + words.shape[1]],
                    lhsT=w1_codes[:, t * P : (t + 1) * P].bitcast(FP8X4),
                    lhsT_scale=w1_scale[:, t * P : (t + 1) * P],
                    rhs=words.bitcast(FP8X4),
                    rhs_scale=xs_placed[:, c0 + at : c0 + at + words.shape[1]],
                    start=True,
                    stop=True,
                )
                at += words.shape[1]
            copy(h[t][:, c0 : c0 + width], acc[:])

        quarters = (xw_half[:, 0:QUARTER], xw_half[:, QUARTER : 2 * QUARTER], xw_third[:], xw_fourth[:])
        for a, words in enumerate(quarters):
            project(0, a * QUARTER, (words,), a, nc.scalar.copy)
        for t in range(1, PACK):
            bank = (2 * t + 2) % 8
            project(t, 0, (xw_half[:],), bank, nc.scalar.copy)
            project(t, BANK, quarters[2:], bank + 1, nc.scalar.copy)

        z_codes = sb.tile([P, V], I32, name="z_codes", align_bytes=64)
        z_scale = sb.tile([P, V], U8, name="z_scale", align_bytes=64)
        out_codes = sb.tile([P, V], I32, name="out_codes", align_bytes=64)
        out_rows = out_0.rearrange("(p t) v -> p t v", t=PACK)
        out_words = out_1[0].rearrange("p n t -> p (n t)").bitcast(I32)
        sums = {}

        def entries(side, c0, n):
            return side[:, c0 // LIST : (c0 + n) // LIST]

        def fetch_v(buffer, t, side, c0):
            nc.vector.tensor_copy(buffer, h[t][:].indirect(entries(side, c0, buffer.shape[1])))

        def fetch_s(buffer, t, side, c0):
            nc.scalar.activation(buffer, h[t][:].indirect(entries(side, c0, buffer.shape[1])), COPY)

        def fetch_sub(out, t, c0, fetched):
            nc.vector.tensor_tensor(out, h[t][:].indirect(entries(left_list, c0, out.shape[1])), fetched, SUB)

        def magnitude(z, d):
            nc.scalar.activation(
                z.rearrange("p (c i) t -> p c t i", i=RUN), d.rearrange("p t (c i) -> p c t i", i=RUN), ABS
            )

        def second_product(e, z):
            c0, n = PIECES[e]
            banks = OUT_BANKS[e]
            nc.vector.quantize_mx(
                out=z_codes[:, c0 : c0 + n].bitcast(FP8X4),
                scales=z_scale[:, c0 : c0 + n],
                in_=z.rearrange("p c t -> p (c t)"),
            )
            width = max(n, GROUP)
            moving = slice(c0 + n - width, c0 + n)
            per_bank = PACK // len(banks)
            accs = [ps.tile([P, per_bank, width], F32, name="acc_out", tag=f"bank{bank}") for bank in banks]
            for t in range(PACK):
                nc.tensor.matmul_mx(
                    out=accs[t // per_bank][:, t % per_bank, :],
                    lhsT=w2_codes[:, 2 * t * P : 2 * (t + 1) * P].bitcast(FP4X4),
                    lhsT_scale=w2_scale[:, t * P : (t + 1) * P],
                    rhs=z_codes[:, moving].bitcast(FP8X4),
                    rhs_scale=z_scale[:, moving],
                    start=True,
                    stop=True,
                )
            sums[e] = [acc[:, :, width - n : width] for acc in accs]

        def round_from_sbuf(interleaved, planes):
            nc.vector.tensor_copy(
                interleaved.rearrange("p (c i) t -> p c t i", i=RUN), planes.rearrange("p t (c i) -> p c t i", i=RUN)
            )

        def quantise_result(c0, interleaved):
            c1 = c0 + interleaved.shape[1]
            nc.vector.quantize_mx(
                out=out_codes[:, c0:c1].bitcast(FP8X4),
                scales=out_scale[:, c0:c1],
                in_=interleaved.rearrange("p c t -> p (c t)"),
            )

        def store_words(c0, c1):
            nc.sync.dma_start(out_words[:, c0:c1], out_codes[:, c0:c1])

        out_scale = sb.tile([P, V], U8, name="out_scale", align_bytes=64)
        top = PACK - 1
        row = GROUP * 4

        def placed(name, shape, dtype, at):
            return turns.tile(shape, dtype, name=name, offset=at * row, align_bytes=64)

        diff0 = placed("diff0", [P, PACK, GROUP], F32, 0)
        diff1 = placed("diff1", [P, PACK, GROUP], F32, 4)
        top_right = [placed("top_right0", [P, GROUP], F32, 12), sb.tile([P, GROUP], F32, name="top_right1")]
        rows = placed("rows", [P, 8, GROUP], F32, 8)
        diff3 = placed("diff3", [P, PACK, GROUP], F32, 4)
        right3 = [placed(f"right3_{t}", [P, GROUP], F32, t) for t in range(PACK)]
        diff = [diff0[:], diff1[:], rows[:, PACK:, :], diff3[:]]
        first = rows[:].rearrange("p (t g) c -> p t (g c)", t=PACK)
        z_bf = [sb.tile([P, n, PACK], BF16, name=f"z_bf{e}", align_bytes=64) for e, (c0, n) in enumerate(PIECES)]
        rounded = [placed("rounded0", [P, WIDE, PACK], BF16, 4)] + [
            sb.tile([P, GROUP, PACK], BF16, name=f"rounded{e}", align_bytes=64) for e in (1, 2)
        ]
        middle = sb.tile([P, PACK, GROUP], F32, name="middle")
        last = sb.tile([P, PACK, GROUP], F32, name="last")
        right0 = [sb.tile([P, WIDE], F32, name=f"right0_{t}") for t in range(top)]
        right2 = [sb.tile([P, GROUP], F32, name=f"right2_{t}") for t in range(PACK)]

        def store_pair(b, copy):
            planes = slice(PAIR * b, PAIR * (b + 1))
            copy(first[:, planes, :], sums[0][b])
            nc.sync.dma_start(out_rows[:, planes, 0:WIDE], first[:, planes, :])

        for t in range(top):
            if t < PAIR:
                fetch_v(right0[t][:], t, right_list, 0)
                fetch_v(right2[t][:], t, right_list, WIDE)
            else:
                for g in range(2):
                    fetch_v(right0[t][:, g * GROUP : (g + 1) * GROUP], t, right_list, g * GROUP)
            for g in range(2):
                fetch_sub(diff[g][:, t, :], t, g * GROUP, right0[t][:, g * GROUP : (g + 1) * GROUP])
        fetch_s(right2[2][:], 2, right_list, WIDE)
        for g in range(2):
            fetch_s(top_right[g][:], top, right_list, g * GROUP)
        fetch_s(right2[top][:], top, right_list, WIDE)
        for g in range(2):
            fetch_sub(diff[g][:, top, :], top, g * GROUP, top_right[g][:])
            magnitude(z_bf[0][:, g * GROUP : (g + 1) * GROUP, :], diff[g])
        for t in range(PACK):
            fetch_sub(diff[2][:, t, :], t, WIDE, right2[t][:])
        fetch_v(right3[top][:], top, right_list, 3 * GROUP)
        second_product(0, z_bf[0][:])
        for t in (0, 2, 1):
            fetch_s(right3[t][:], t, right_list, 3 * GROUP)
        magnitude(z_bf[1][:], diff[2])
        store_pair(0, nc.scalar.copy)
        for t in (3, 0, 2, 1):
            fetch_sub(diff[3][:, t, :], t, 3 * GROUP, right3[t][:])
        second_product(1, z_bf[1][:])
        magnitude(z_bf[2][:], diff[3])
        store_pair(1, nc.vector.tensor_copy)
        second_product(2, z_bf[2][:])
        nc.scalar.copy(middle[:], sums[1][0])
        nc.sync.dma_start(out_rows[:, :, WIDE : WIDE + GROUP], middle[:])
        for b in range(2):
            nc.scalar.copy(last[:, PAIR * b : PAIR * (b + 1), :], sums[2][b])
        nc.sync.dma_start(out_rows[:, :, WIDE + GROUP :], last[:])
        round_from_sbuf(rounded[0][:], first)
        round_from_sbuf(rounded[1][:], middle[:])
        quantise_result(0, rounded[0][:])
        store_words(0, WIDE)
        round_from_sbuf(rounded[2][:], last[:])
        quantise_result(WIDE, rounded[1][:])
        quantise_result(WIDE + GROUP, rounded[2][:])
        store_words(WIDE, V)

        for q in range(QUADRANTS):
            queue = (nc.sync, nc.scalar)[q % 2]
            queue.dma_start(
                out_2[0][4 * q : 4 * q + 4, :].bitcast(I32), out_scale[32 * q : 32 * q + 4, :].bitcast(I32)
            )
